import numpy as np
import ml_dtypes


def mxq(x, axis, fmt="e4m3"):
    dtype, down = {"e4m3": (ml_dtypes.float8_e4m3fn, 7), "e5m2": (ml_dtypes.float8_e5m2, 14)}[fmt]
    v = np.moveaxis(np.asarray(x, np.float32).astype(ml_dtypes.bfloat16).astype(np.float64), axis, -1)
    blocks = v.reshape(v.shape[:-1] + (-1, 32))
    amax = np.abs(blocks).max(-1, keepdims=True)
    byte = np.maximum(np.where(amax > 0, np.frexp(amax)[1] - 1 + 127, 0) - down, 1)
    scale = np.exp2(byte - 127.0)
    codes = (blocks / scale).astype(np.float32).astype(dtype).astype(np.float64)
    return np.moveaxis((codes * scale).reshape(v.shape), -1, axis)


WIDE = False


def mx_kscale(k):
    if not WIDE:
        return np.ones(k)
    levels = np.array([10, -10, 5, -5, 0])
    if k % 512:
        return np.exp2(np.random.permutation(np.resize(levels, k // 32))).repeat(32)
    a = np.empty((k // 512, 16))
    for p in range(k // 512):
        a[p, :8] = np.random.permutation(np.resize(levels, 8))
        for g in range(8):
            far = levels[np.abs(levels - a[p, g]) >= 10]
            a[p, g + 8] = far[np.random.randint(len(far))]
    return np.exp2(a.ravel()).repeat(32)


def f64(x):
    return np.asarray(x).astype(np.float64)


def striped(idx):
    return np.tile(idx.reshape(-1, 16).T, (8, 1)).astype(np.uint16)


def unstriped(offs):
    return offs[:16].T.reshape(-1).astype(np.int64)


def pack_weight(w):
    k, n = w.shape
    w = f64(np.asarray(w, np.float32).astype(ml_dtypes.bfloat16)).reshape(k // 32, 32, n)
    amax = np.abs(w).max(1)
    byte = np.clip(np.where(amax > 0, np.frexp(amax)[1] - 1 + 127 - 7, 1), 1, 254)
    scaled = (w * np.exp2(127.0 - byte)[:, None, :]).reshape(k, n).astype(np.float32)
    words = np.ascontiguousarray(scaled.reshape(k // 512, 128, 4, n).transpose(0, 1, 3, 2)).astype(ml_dtypes.float8_e4m3fn).view(np.uint8)
    return words, np.ascontiguousarray(byte.astype(np.uint8).reshape(k // 512, 16, n))


def unpack_weight(words, scales):
    g, p, n, _ = words.shape
    vals = np.ascontiguousarray(words).view(ml_dtypes.float8_e4m3fn).astype(np.float64) * np.repeat(np.exp2(scales.astype(np.float64) - 127.0), 8, axis=1)[..., None]
    return vals.transpose(0, 1, 3, 2).reshape(g * 512, n)


def sigmoid(v):
    return 1.0 / (1.0 + np.exp(-np.maximum(v, -700.0)))


K, T, S, D, V, H, G, R = 512, 1024, 512, 3, 256, 512, 2048, 512
P = 2 ** 7


def setup_inputs():
    n = np.random.standard_normal
    s = mx_kscale(K)[:, None]
    u = mx_kscale(H)
    near = np.random.permutation(S)
    packed_xT = pack_weight(n((K, T)) * s)
    packed_vT = pack_weight(n((H, G)) / np.sqrt(H) / u[:, None])
    return {
        "x_words": packed_xT[0],
        "x_scales": packed_xT[1],
        "w1": (n((K, H)) / np.sqrt(K) / s * u).astype(np.float32),
        "gate": (np.tile(np.random.uniform(0.2, 1.0, (D, 1, V)) / np.sqrt(D), (1, P, 1))).astype(np.float32),
        "v_words": packed_vT[0],
        "v_scales": packed_vT[1],
        "offs": striped(np.random.permutation(T)[:S]),
        "pos1": striped(near[:V]),
        "pos2": striped(near[V:]),
        "pos3": striped(np.random.permutation(S)[:V]),
        "cand": striped(np.random.permutation(G)[:R]),
    }


def reference(x_words, x_scales, w1, gate, v_words, v_scales, offs, pos1, pos2, pos3, cand):
    xq = unpack_weight(x_words, x_scales)[:, unstriped(offs)]
    h = mxq(f64(w1), 0, "e4m3").T @ xq
    z = h[:, unstriped(pos1)] * f64(gate)[0, :1] + h[:, unstriped(pos2)] * f64(gate)[1, :1] + h[:, unstriped(pos3)] * f64(gate)[2, :1]
    v_cand = unpack_weight(v_words, v_scales)[:, unstriped(cand)]
    y = mxq(z, 0, "e4m3").T @ v_cand
    return sigmoid(y)

@@ -1,0 +1,182 @@
+from contextlib import ExitStack
+
+import concourse.mybir as mybir
+from concourse.masks import make_identity
+
+K, T, S, D, V, H, G, R = 512, 1024, 512, 3, 256, 512, 2048, 512
+FLOPS = 2 * K * H * S + 2 * H * V * R
+
+F32 = mybir.dt.float32
+BF16 = mybir.dt.bfloat16
+I32 = mybir.dt.int32
+U32 = mybir.dt.uint32
+U16 = mybir.dt.uint16
+U8 = mybir.dt.uint8
+FP8X4 = mybir.dt.float8_e4m3fn_x4
+MULT = mybir.AluOpType.mult
+SIGMOID = mybir.ActivationFunctionType.Sigmoid
+
+P = 128
+PACK = 4
+ROW_TILES = H // P
+HALF = 256
+
+
+def load_scale_rows(queue, plane, scales):
+    for q in range(4):
+        queue.dma_start(out=plane[32 * q : 32 * q + 4, :].bitcast(I32), in_=scales[0, 4 * q : 4 * q + 4, :].bitcast(I32))
+
+
+def tile_picked_zcbow_sig_p_kernel(
+    tc, x_words, x_scales, w1, gate, v_words, v_scales, offs, pos1, pos2, pos3, cand, out
+):
+    nc = tc.nc
+    with ExitStack() as ctx:
+        keep = ctx.enter_context(tc.tile_pool(name="keep", bufs=1))
+        psum = ctx.enter_context(tc.psum_pool(name="psum", bufs=1))
+
+        def bank(number, shape, name):
+            return psum.tile(shape, F32, name=name, tag=f"bank{number}")
+
+        def product(acc, codes, plane, moving, moving_plane):
+            nc.tensor.matmul_mx(
+                out=acc,
+                lhsT=codes.bitcast(FP8X4),
+                lhsT_scale=plane,
+                rhs=moving.bitcast(FP8X4),
+                rhs_scale=moving_plane,
+                start=True,
+                stop=True,
+            )
+
+        offs_t = keep.tile([P, S // 16], U16, name="offs_t")
+        cand_t = keep.tile([P, R // 16], U16, name="cand_t")
+        pos_t = [keep.tile([P, V // 16], U16, name=f"pos_t{d}") for d in range(D)]
+        xw = keep.tile([P, T], U32, name="xw", align_bytes=64)
+        xs = keep.tile([P, T], U8, name="xs", align_bytes=64)
+        vw = keep.tile([P, G], U32, name="vw", align_bytes=64)
+        vs = keep.tile([P, G], U8, name="vs", tag="vs", align_bytes=64)
+        gate_t = keep.tile([P, D, V], F32, name="gate_t")
+        w_first = keep.tile([P, PACK, HALF], F32, name="w_first")
+        w_rest = keep.tile([P, PACK, HALF], F32, name="w_rest")
+        ident = keep.tile([P, P], F32, name="ident")
+        warm = keep.tile([P, 8], F32, name="warm")
+
+        nc.vector.memset(xs[:].bitcast(I32), 0)
+        nc.vector.memset(vs[:].bitcast(I32), 0)
+        nc.gpsimd.memset(warm[:], 0.0)
+        make_identity(nc, ident[:])
+
+        w_rows = w1.rearrange("(p j) c -> p j c", j=PACK)
+        nc.sync.dma_start(out=offs_t[:], in_=offs)
+        nc.sync.dma_start(out=xw[:].bitcast(I32), in_=x_words[0].rearrange("p n t -> p (n t)").bitcast(I32))
+        load_scale_rows(nc.sync, xs, x_scales)
+        nc.sync.dma_start(out=w_first[:], in_=w_rows[:, :, 0:HALF])
+        nc.sync.dma_start(out=cand_t[:], in_=cand)
+        nc.sync.dma_start(out=gate_t[:], in_=gate.rearrange("d p t -> p d t"))
+        load_scale_rows(nc.sync, vs, v_scales)
+        for d, pos in enumerate((pos1, pos2, pos3)):
+            nc.sync.dma_start(out=pos_t[d][:], in_=pos)
+        nc.sync.dma_start(out=w_rest[:], in_=w_rows[:, :, HALF:H])
+        nc.sync.dma_start(out=vw[:].bitcast(I32), in_=v_words[0].rearrange("p n t -> p (n t)").bitcast(I32))
+
+        nc.scalar.activation(out=warm[:, 1:2], in_=warm[:, 0:1], func=SIGMOID)
+
+
+        xg_s = keep.tile([P, S], U8, name="xg_s", align_bytes=64)
+        xg_all = keep.tile([P, S], U32, name="xg_all", align_bytes=64)
+        nc.vector.tensor_copy(out=xg_all[:], in_=xw[:].indirect(offs_t[:]))
+        nc.vector.tensor_copy(out=xg_s[:], in_=xs[:].indirect(offs_t[:]))
+
+        def quantise_w(m):
+            raw = (w_first, w_rest)[m // 2][:, :, (m % 2) * P : (m % 2 + 1) * P]
+            grouped = keep.tile([P, P, PACK], BF16, name=f"w_grouped{m}", align_bytes=64)
+            nc.scalar.copy(out=grouped[:], in_=raw.rearrange("p j c -> p c j"))
+            codes = keep.tile([P, P], U32, name=f"w_codes{m}", align_bytes=64)
+            plane = keep.tile([P, P], U8, name=f"w_plane{m}", align_bytes=64)
+            nc.vector.quantize_mx(out=codes[:].bitcast(FP8X4), scales=plane[:], in_=grouped[:].rearrange("p c j -> p (c j)"))
+            return codes, plane
+
+        h = [keep.tile([P, S], F32, name=f"h{m}", tag=f"h{m}", align_bytes=64) for m in range(ROW_TILES)]
+        codes, plane = quantise_w(0)
+        for a in range(2):
+            cols = slice(a * HALF, (a + 1) * HALF)
+            h_ps = bank(a, [P, HALF], f"h_ps0_{a}")
+            product(h_ps[:], codes[:], plane[:], xg_all[:, cols], xg_s[:, cols])
+            nc.scalar.copy(out=h[0][:, cols], in_=h_ps[:])
+
+        def project(m):
+            codes, plane = quantise_w(m)
+            h_ps = bank((m + 1) % 3, [P, S], f"h_ps{m}")
+            product(h_ps[:], codes[:], plane[:], xg_all[:], xg_s[:])
+            nc.scalar.copy(out=h[m][:], in_=h_ps[:])
+
+        zt = [keep.tile([P, 2, P, 2], BF16, name=f"zt{b}", align_bytes=64) for b in range(2)]
+
+        def windows(m, blocks, number, tags):
+            n = len(blocks)
+            zt_ps = bank(number, [P, n, P], f"zt_ps{m}_{blocks[0]}")
+            cols = slice(blocks[0] * P, (blocks[-1] + 1) * P)
+            entries = slice(blocks[0] * 8, (blocks[-1] + 1) * 8)
+            for d in range(D):
+                term = keep.tile([P, n * P], F32, name=f"term{m}_{d}_{blocks[0]}", tag=tags[d], align_bytes=64)
+                nc.vector.tensor_tensor(
+                    out=term[:], in0=h[m][:].indirect(pos_t[d][:, entries]), in1=gate_t[:, d, cols], op=MULT
+                )
+                for a in range(n):
+                    nc.tensor.matmul(
+                        out=zt_ps[:, a, :],
+                        lhsT=term[:, a * P : (a + 1) * P],
+                        rhs=ident[:],
+                        is_transpose=True,
+                        start=(d == 0 and a == 0),
+                        stop=(d == D - 1 and a == n - 1),
+                    )
+            for a in range(n):
+                nc.scalar.copy(
+                    out=zt[blocks[a]][:, :, 32 * m : 32 * (m + 1), :],
+                    in_=zt_ps[:, a, :].rearrange("t (p u e) -> t u p e", u=2, e=2),
+                )
+
+        def quantise_z(b):
+            zt_words = zt[b][:].rearrange("t u p e -> t (u p e)").bitcast(F32)
+            z_ps = bank(b, [P, 2, P], f"z_ps{b}")
+            for u in range(2):
+                nc.tensor.transpose(z_ps[:, u, :], zt_words[:, u * P : (u + 1) * P], ident[:])
+            z_grouped = keep.tile([P, P, PACK], BF16, name=f"z_grouped{b}", align_bytes=64)
+            z_flat = z_grouped[:].rearrange("p t j -> p (t j)")
+            nc.scalar.copy(
+                out=z_flat.bitcast(F32).rearrange("p (t u) -> p t u", u=2), in_=z_ps[:].rearrange("p u t -> p t u")
+            )
+            z_codes = keep.tile([P, P], U32, name=f"z_codes{b}", align_bytes=64)
+            z_plane = keep.tile([P, P], U8, name=f"z_plane{b}", align_bytes=64)
+            nc.vector.quantize_mx(out=z_codes[:].bitcast(FP8X4), scales=z_plane[:], in_=z_flat)
+            return z_codes, z_plane
+
+        vg_s = keep.tile([P, R], U8, name="vg_s", align_bytes=64)
+        nc.vector.tensor_copy(out=vg_s[:], in_=vs[:].indirect(cand_t[:]))
+        project(1)
+        windows(0, [0, 1], 3, ["vs", "t01", "t02"])
+        project(2)
+        project(3)
+        windows(1, [0, 1], 4, ["t10", "t11", "t12"])
+        windows(2, [0], 3, ["t20", "t21", "t22"])
+        windows(3, [0], 4, ["t30", "t31", "t32"])
+        windows(2, [1], 5, ["t30", "t41", "t42"])
+        z0 = quantise_z(0)
+        windows(3, [1], 3, ["t50", "t51", "t52"])
+        vg_w = keep.tile([P, R], U32, name="vg_w", tag="h2", align_bytes=64)
+        nc.vector.tensor_copy(out=vg_w[:], in_=vw[:].indirect(cand_t[:]))
+        y_ps = bank(2, [P, R], "y_ps0")
+        product(y_ps[:], z0[0][:], z0[1][:], vg_w[:], vg_s[:])
+        z1 = quantise_z(1)
+        result = keep.tile([P, R], F32, name="result0")
+        nc.scalar.activation(out=result[:], in_=y_ps[:], func=SIGMOID)
+        nc.sync.dma_start(out=out[0:P, :], in_=result[:])
+        for a in range(2):
+            cols = slice(a * HALF, (a + 1) * HALF)
+            y_half = bank(6 + a, [P, HALF], f"y_ps1_{a}")
+            product(y_half[:], z1[0][:], z1[1][:], vg_w[:, cols], vg_s[:, cols])
+            part = keep.tile([P, HALF], F32, name=f"result1_{a}")
+            nc.scalar.activation(out=part[:], in_=y_half[:], func=SIGMOID)
+            nc.sync.dma_start(out=out[P : 2 * P, cols], in_=part[:])

@@ -18,13 +18,27 @@ SIGMOID = mybir.ActivationFunctionType.Sigmoid
 
 P = 128
 PACK = 4
+QUADRANT = 32
+LIST_ROWS = 16
 ROW_TILES = H // P
 HALF = 256
+HALVES = (slice(0, HALF), slice(HALF, 2 * HALF))
 
 
-def load_scale_rows(queue, plane, scales):
-    for q in range(4):
-        queue.dma_start(out=plane[32 * q : 32 * q + 4, :].bitcast(I32), in_=scales[0, 4 * q : 4 * q + 4, :].bitcast(I32))
+def load_words(nc, tile, words):
+    nc.sync.dma_start(out=tile[:].bitcast(I32), in_=words[0].rearrange("p n t -> p (n t)").bitcast(I32))
+
+
+def load_scale_rows(nc, plane, scales):
+    for q in range(P // QUADRANT):
+        nc.sync.dma_start(
+            out=plane[QUADRANT * q : QUADRANT * q + PACK, :].bitcast(I32),
+            in_=scales[0, PACK * q : PACK * (q + 1), :].bitcast(I32),
+        )
+
+
+def entries(offsets, cols):
+    return offsets[:, cols.start // LIST_ROWS : cols.stop // LIST_ROWS]
 
 
 def tile_picked_zcbow_sig_p_kernel(
@@ -34,6 +48,9 @@ def tile_picked_zcbow_sig_p_kernel(
     with ExitStack() as ctx:
         keep = ctx.enter_context(tc.tile_pool(name="keep", bufs=1))
         psum = ctx.enter_context(tc.psum_pool(name="psum", bufs=1))
+
+        def sbuf(name, shape, dtype, after=None):
+            return keep.tile(shape, dtype, name=name, tag=after or name, align_bytes=64)
 
         def bank(number, shape, name):
             return psum.tile(shape, F32, name=name, tag=f"bank{number}")
@@ -49,134 +66,150 @@ def tile_picked_zcbow_sig_p_kernel(
                 stop=True,
             )
 
-        offs_t = keep.tile([P, S // 16], U16, name="offs_t")
-        cand_t = keep.tile([P, R // 16], U16, name="cand_t")
-        pos_t = [keep.tile([P, V // 16], U16, name=f"pos_t{d}") for d in range(D)]
-        xw = keep.tile([P, T], U32, name="xw", align_bytes=64)
-        xs = keep.tile([P, T], U8, name="xs", align_bytes=64)
-        vw = keep.tile([P, G], U32, name="vw", align_bytes=64)
-        vs = keep.tile([P, G], U8, name="vs", tag="vs", align_bytes=64)
-        gate_t = keep.tile([P, D, V], F32, name="gate_t")
-        w_first = keep.tile([P, PACK, HALF], F32, name="w_first")
-        w_rest = keep.tile([P, PACK, HALF], F32, name="w_rest")
-        ident = keep.tile([P, P], F32, name="ident")
-        warm = keep.tile([P, 8], F32, name="warm")
+        def quantise(name, grouped):
+            codes = sbuf(f"{name}_codes", [P, P], U32)
+            plane = sbuf(f"{name}_plane", [P, P], U8)
+            nc.vector.quantize_mx(
+                out=codes[:].bitcast(FP8X4), scales=plane[:], in_=grouped[:].rearrange("p c j -> p (c j)")
+            )
+            return codes[:], plane[:]
 
-        nc.vector.memset(xs[:].bitcast(I32), 0)
-        nc.vector.memset(vs[:].bitcast(I32), 0)
+        offs_t = sbuf("offs_t", [P, S // LIST_ROWS], U16)
+        cand_t = sbuf("cand_t", [P, R // LIST_ROWS], U16)
+        pos_t = [sbuf(f"pos_t{d}", [P, V // LIST_ROWS], U16) for d in range(D)]
+        x_table = sbuf("x_table", [P, T], U32)
+        x_table_plane = sbuf("x_table_plane", [P, T], U8)
+        v_table = sbuf("v_table", [P, G], U32)
+        v_table_plane = sbuf("v_table_plane", [P, G], U8)
+        gate_t = sbuf("gate_t", [P, D, V], F32)
+        w_raw0 = sbuf("w_raw0", [P, PACK, P], F32)
+        w_raw1 = sbuf("w_raw1", [P, PACK, P], F32)
+        w_raw23 = sbuf("w_raw23", [P, PACK, 2 * P], F32)
+        ident = sbuf("ident", [P, P], F32)
+        warm = sbuf("warm", [P, 8], F32)
+
+        nc.vector.memset(x_table_plane[:].bitcast(I32), 0)
+        nc.vector.memset(v_table_plane[:].bitcast(I32), 0)
         nc.gpsimd.memset(warm[:], 0.0)
         make_identity(nc, ident[:])
 
         w_rows = w1.rearrange("(p j) c -> p j c", j=PACK)
         nc.sync.dma_start(out=offs_t[:], in_=offs)
-        nc.sync.dma_start(out=xw[:].bitcast(I32), in_=x_words[0].rearrange("p n t -> p (n t)").bitcast(I32))
-        load_scale_rows(nc.sync, xs, x_scales)
-        nc.sync.dma_start(out=w_first[:], in_=w_rows[:, :, 0:HALF])
+        load_words(nc, x_table, x_words)
+        load_scale_rows(nc, x_table_plane, x_scales)
+        nc.sync.dma_start(out=w_raw0[:], in_=w_rows[:, :, 0:P])
         nc.sync.dma_start(out=cand_t[:], in_=cand)
+        nc.sync.dma_start(out=w_raw1[:], in_=w_rows[:, :, P : 2 * P])
+        load_scale_rows(nc, v_table_plane, v_scales)
         nc.sync.dma_start(out=gate_t[:], in_=gate.rearrange("d p t -> p d t"))
-        load_scale_rows(nc.sync, vs, v_scales)
-        for d, pos in enumerate((pos1, pos2, pos3)):
-            nc.sync.dma_start(out=pos_t[d][:], in_=pos)
-        nc.sync.dma_start(out=w_rest[:], in_=w_rows[:, :, HALF:H])
-        nc.sync.dma_start(out=vw[:].bitcast(I32), in_=v_words[0].rearrange("p n t -> p (n t)").bitcast(I32))
+        nc.sync.dma_start(out=pos_t[0][:], in_=pos1)
+        nc.sync.dma_start(out=w_raw23[:], in_=w_rows[:, :, 2 * P : H])
+        nc.sync.dma_start(out=pos_t[1][:], in_=pos2)
+        nc.sync.dma_start(out=pos_t[2][:], in_=pos3)
+        load_words(nc, v_table, v_words)
 
         nc.scalar.activation(out=warm[:, 1:2], in_=warm[:, 0:1], func=SIGMOID)
 
-
-        xg_s = keep.tile([P, S], U8, name="xg_s", align_bytes=64)
-        xg_all = keep.tile([P, S], U32, name="xg_all", align_bytes=64)
-        nc.vector.tensor_copy(out=xg_all[:], in_=xw[:].indirect(offs_t[:]))
-        nc.vector.tensor_copy(out=xg_s[:], in_=xs[:].indirect(offs_t[:]))
-
-        def quantise_w(m):
-            raw = (w_first, w_rest)[m // 2][:, :, (m % 2) * P : (m % 2 + 1) * P]
-            grouped = keep.tile([P, P, PACK], BF16, name=f"w_grouped{m}", align_bytes=64)
+        def cast_w(m, raw, after=None):
+            grouped = sbuf(f"w_grouped{m}", [P, P, PACK], BF16, after)
             nc.scalar.copy(out=grouped[:], in_=raw.rearrange("p j c -> p c j"))
-            codes = keep.tile([P, P], U32, name=f"w_codes{m}", align_bytes=64)
-            plane = keep.tile([P, P], U8, name=f"w_plane{m}", align_bytes=64)
-            nc.vector.quantize_mx(out=codes[:].bitcast(FP8X4), scales=plane[:], in_=grouped[:].rearrange("p c j -> p (c j)"))
-            return codes, plane
+            return grouped
 
-        h = [keep.tile([P, S], F32, name=f"h{m}", tag=f"h{m}", align_bytes=64) for m in range(ROW_TILES)]
-        codes, plane = quantise_w(0)
-        for a in range(2):
-            cols = slice(a * HALF, (a + 1) * HALF)
+        h = [sbuf(f"h{m}", [P, S], F32) for m in range(ROW_TILES)]
+        x_codes = sbuf("x_codes", [P, S], U32)
+        nc.vector.tensor_copy(out=x_codes[:], in_=x_table[:].indirect(offs_t[:]))
+        x_planes = [sbuf("x_plane0", [P, HALF], U8), sbuf("x_plane1", [P, HALF], U8, "w_raw0")]
+        nc.vector.tensor_copy(out=x_planes[0][:], in_=x_table_plane[:].indirect(entries(offs_t, HALVES[0])))
+        w0 = quantise("w0", cast_w(0, w_raw0[:]))
+        nc.vector.tensor_copy(out=x_planes[1][:], in_=x_table_plane[:].indirect(entries(offs_t, HALVES[1])))
+        for a, cols in enumerate(HALVES):
             h_ps = bank(a, [P, HALF], f"h_ps0_{a}")
-            product(h_ps[:], codes[:], plane[:], xg_all[:, cols], xg_s[:, cols])
+            product(h_ps[:], *w0, x_codes[:, cols], x_planes[a][:])
             nc.scalar.copy(out=h[0][:, cols], in_=h_ps[:])
 
-        def project(m):
-            codes, plane = quantise_w(m)
-            h_ps = bank((m + 1) % 3, [P, S], f"h_ps{m}")
-            product(h_ps[:], codes[:], plane[:], xg_all[:], xg_s[:])
-            nc.scalar.copy(out=h[m][:], in_=h_ps[:])
+        def project(m, number, grouped):
+            w_m = quantise(f"w{m}", grouped)
+            h_ps = bank(number, [P, S], f"h_ps{m}")
+            for a, cols in enumerate(HALVES):
+                product(h_ps[:, cols], *w_m, x_codes[:, cols], x_planes[a][:])
+            return h_ps
 
-        zt = [keep.tile([P, 2, P, 2], BF16, name=f"zt{b}", align_bytes=64) for b in range(2)]
+        zt = [sbuf(f"zt{b}", [P, 2, P, 2], BF16) for b in range(V // P)]
 
-        def windows(m, blocks, number, tags):
+        def windows(m, blocks, number, terms, before_last=None):
             n = len(blocks)
             zt_ps = bank(number, [P, n, P], f"zt_ps{m}_{blocks[0]}")
             cols = slice(blocks[0] * P, (blocks[-1] + 1) * P)
-            entries = slice(blocks[0] * 8, (blocks[-1] + 1) * 8)
             for d in range(D):
-                term = keep.tile([P, n * P], F32, name=f"term{m}_{d}_{blocks[0]}", tag=tags[d], align_bytes=64)
+                if d == D - 1 and before_last is not None:
+                    before_last()
                 nc.vector.tensor_tensor(
-                    out=term[:], in0=h[m][:].indirect(pos_t[d][:, entries]), in1=gate_t[:, d, cols], op=MULT
+                    out=terms[d], in0=h[m][:].indirect(entries(pos_t[d], cols)), in1=gate_t[:, d, cols], op=MULT
                 )
                 for a in range(n):
                     nc.tensor.matmul(
                         out=zt_ps[:, a, :],
-                        lhsT=term[:, a * P : (a + 1) * P],
+                        lhsT=terms[d][:, a * P : (a + 1) * P],
                         rhs=ident[:],
                         is_transpose=True,
                         start=(d == 0 and a == 0),
                         stop=(d == D - 1 and a == n - 1),
                     )
+            words_here = slice(m * P // PACK, (m + 1) * P // PACK)
             for a in range(n):
                 nc.scalar.copy(
-                    out=zt[blocks[a]][:, :, 32 * m : 32 * (m + 1), :],
+                    out=zt[blocks[a]][:, :, words_here, :],
                     in_=zt_ps[:, a, :].rearrange("t (p u e) -> t u p e", u=2, e=2),
                 )
 
-        def quantise_z(b):
-            zt_words = zt[b][:].rearrange("t u p e -> t (u p e)").bitcast(F32)
-            z_ps = bank(b, [P, 2, P], f"z_ps{b}")
+        def turn_z(b, number):
+            pairs = zt[b][:].rearrange("t u p e -> t (u p e)").bitcast(F32)
+            z_ps = bank(number, [P, 2, P], f"z_ps{b}")
             for u in range(2):
-                nc.tensor.transpose(z_ps[:, u, :], zt_words[:, u * P : (u + 1) * P], ident[:])
-            z_grouped = keep.tile([P, P, PACK], BF16, name=f"z_grouped{b}", align_bytes=64)
-            z_flat = z_grouped[:].rearrange("p t j -> p (t j)")
-            nc.scalar.copy(
-                out=z_flat.bitcast(F32).rearrange("p (t u) -> p t u", u=2), in_=z_ps[:].rearrange("p u t -> p t u")
-            )
-            z_codes = keep.tile([P, P], U32, name=f"z_codes{b}", align_bytes=64)
-            z_plane = keep.tile([P, P], U8, name=f"z_plane{b}", align_bytes=64)
-            nc.vector.quantize_mx(out=z_codes[:].bitcast(FP8X4), scales=z_plane[:], in_=z_flat)
-            return z_codes, z_plane
+                nc.tensor.transpose(z_ps[:, u, :], pairs[:, u * P : (u + 1) * P], ident[:])
+            grouped = sbuf(f"z_grouped{b}", [P, P, PACK], BF16)
+            grouped_pairs = grouped[:].rearrange("p t j -> p (t j)").bitcast(F32).rearrange("p (t u) -> p t u", u=2)
+            nc.scalar.copy(out=grouped_pairs, in_=z_ps[:].rearrange("p u t -> p t u"))
+            return grouped
 
-        vg_s = keep.tile([P, R], U8, name="vg_s", align_bytes=64)
-        nc.vector.tensor_copy(out=vg_s[:], in_=vs[:].indirect(cand_t[:]))
-        project(1)
-        windows(0, [0, 1], 3, ["vs", "t01", "t02"])
-        project(2)
-        project(3)
-        windows(1, [0, 1], 4, ["t10", "t11", "t12"])
-        windows(2, [0], 3, ["t20", "t21", "t22"])
-        windows(3, [0], 4, ["t30", "t31", "t32"])
-        windows(2, [1], 5, ["t30", "t41", "t42"])
-        z0 = quantise_z(0)
-        windows(3, [1], 3, ["t50", "t51", "t52"])
-        vg_w = keep.tile([P, R], U32, name="vg_w", tag="h2", align_bytes=64)
-        nc.vector.tensor_copy(out=vg_w[:], in_=vw[:].indirect(cand_t[:]))
-        y_ps = bank(2, [P, R], "y_ps0")
-        product(y_ps[:], z0[0][:], z0[1][:], vg_w[:], vg_s[:])
-        z1 = quantise_z(1)
-        result = keep.tile([P, R], F32, name="result0")
-        nc.scalar.activation(out=result[:], in_=y_ps[:], func=SIGMOID)
-        nc.sync.dma_start(out=out[0:P, :], in_=result[:])
-        for a in range(2):
-            cols = slice(a * HALF, (a + 1) * HALF)
-            y_half = bank(6 + a, [P, HALF], f"y_ps1_{a}")
-            product(y_half[:], z1[0][:], z1[1][:], vg_w[:, cols], vg_s[:, cols])
-            part = keep.tile([P, HALF], F32, name=f"result1_{a}")
-            nc.scalar.activation(out=part[:], in_=y_half[:], func=SIGMOID)
-            nc.sync.dma_start(out=out[P : 2 * P, cols], in_=part[:])
+        v_plane = sbuf("v_plane", [P, R], U8, "w_grouped0")
+        nc.vector.tensor_copy(out=v_plane[:], in_=v_table_plane[:].indirect(cand_t[:]))
+
+        h_ps1 = project(1, 3, cast_w(1, w_raw1[:]))
+        grouped2 = cast_w(2, w_raw23[:, :, 0:P], "w0_codes")
+        grouped3 = cast_w(3, w_raw23[:, :, P : 2 * P], "w0_plane")
+        nc.scalar.copy(out=h[1][:], in_=h_ps1[:])
+
+        def project_rest():
+            nc.scalar.copy(out=h[2][:], in_=project(2, 0, grouped2)[:])
+            nc.scalar.copy(out=h[3][:], in_=project(3, 1, grouped3)[:])
+
+        first_terms = [sbuf(f"term0_{d}", [P, V], F32, "w_raw23" if d == D - 1 else None)[:] for d in range(D)]
+        windows(0, [0, 1], 4, first_terms, project_rest)
+
+        for m in range(1, ROW_TILES):
+            windows(m, [0], 4 + m, [sbuf(f"term{m}_{d}", [P, P], F32)[:] for d in range(D)])
+        late = sbuf("late_terms", [P, (ROW_TILES - 1) * D, P], F32, f"term{ROW_TILES - 1}_0")
+        windows(1, [1], 2, [late[:, d, :] for d in range(D)])
+        z_grouped0 = turn_z(0, 5)
+        windows(2, [1], 3, [late[:, D + d, :] for d in range(D)])
+        windows(3, [1], 4, [late[:, 2 * D + d, :] for d in range(D)])
+        z = [quantise("z0", z_grouped0)]
+
+        v_codes = sbuf("v_codes", [P, R], U32, "z_grouped0")
+        z_grouped1 = turn_z(1, 6)
+
+        def score(b, cols, number, queue, after=None):
+            y_ps = bank(number, [P, HALF], f"y_ps{b}_{cols.start}")
+            product(y_ps[:], *z[b], v_codes[:, cols], v_plane[:, cols])
+            result = sbuf(f"result{b}_{cols.start}", [P, HALF], F32, after)
+            nc.scalar.activation(out=result[:], in_=y_ps[:], func=SIGMOID)
+            queue.dma_start(out=out[b * P : (b + 1) * P, cols], in_=result[:])
+
+        nc.vector.tensor_copy(out=v_codes[:, HALVES[0]], in_=v_table[:].indirect(entries(cand_t, HALVES[0])))
+        score(0, HALVES[0], 4, nc.sync, "zt1")
+        nc.vector.tensor_copy(out=v_codes[:, HALVES[1]], in_=v_table[:].indirect(entries(cand_t, HALVES[1])))
+        score(0, HALVES[1], 0, nc.sync)
+        z.append(quantise("z1", z_grouped1))
+        score(1, HALVES[0], 1, nc.sync)
+        score(1, HALVES[1], 2, nc.scalar)

@@ -14,6 +14,7 @@ U16 = mybir.dt.uint16
 U8 = mybir.dt.uint8
 FP8X4 = mybir.dt.float8_e4m3fn_x4
 MULT = mybir.AluOpType.mult
+ADD = mybir.AluOpType.add
 SIGMOID = mybir.ActivationFunctionType.Sigmoid
 
 P = 128
@@ -34,6 +35,14 @@ def load_scale_rows(nc, plane, scales):
         nc.sync.dma_start(
             out=plane[QUADRANT * q : QUADRANT * q + PACK, :].bitcast(I32),
             in_=scales[0, PACK * q : PACK * (q + 1), :].bitcast(I32),
+        )
+
+
+def load_scale_rows_repeated(nc, plane, scales):
+    for q in range(P // QUADRANT):
+        nc.sync.dma_start(
+            out=plane[QUADRANT * q : QUADRANT * (q + 1), :].bitcast(I32),
+            in_=scales[0, PACK * q : PACK * (q + 1), :].bitcast(I32).partition_broadcast(QUADRANT // PACK),
         )
 
 
@@ -82,81 +91,101 @@ def tile_picked_zcbow_sig_p_kernel(
         v_table = sbuf("v_table", [P, G], U32)
         v_table_plane = sbuf("v_table_plane", [P, G], U8)
         gate_t = sbuf("gate_t", [P, D, V], F32)
-        w_raw0 = sbuf("w_raw0", [P, PACK, P], F32)
-        w_raw1 = sbuf("w_raw1", [P, PACK, P], F32)
-        w_raw23 = sbuf("w_raw23", [P, PACK, 2 * P], F32)
+        w_raw = [sbuf(f"w_raw{m}", [P, PACK, P], F32) for m in range(ROW_TILES)]
         ident = sbuf("ident", [P, P], F32)
         warm = sbuf("warm", [P, 8], F32)
 
-        nc.vector.memset(x_table_plane[:].bitcast(I32), 0)
         nc.vector.memset(v_table_plane[:].bitcast(I32), 0)
         nc.gpsimd.memset(warm[:], 0.0)
         make_identity(nc, ident[:])
 
         w_rows = w1.rearrange("(p j) c -> p j c", j=PACK)
+
+        def load_w(m):
+            nc.sync.dma_start(out=w_raw[m][:], in_=w_rows[:, :, m * P : (m + 1) * P])
+
         nc.sync.dma_start(out=offs_t[:], in_=offs)
-        load_words(nc, x_table, x_words)
-        load_scale_rows(nc, x_table_plane, x_scales)
-        nc.sync.dma_start(out=w_raw0[:], in_=w_rows[:, :, 0:P])
+        load_scale_rows_repeated(nc, x_table_plane, x_scales)
         nc.sync.dma_start(out=cand_t[:], in_=cand)
-        nc.sync.dma_start(out=w_raw1[:], in_=w_rows[:, :, P : 2 * P])
+        load_words(nc, x_table, x_words)
+        load_w(0)
         load_scale_rows(nc, v_table_plane, v_scales)
+        load_w(1)
         nc.sync.dma_start(out=gate_t[:], in_=gate.rearrange("d p t -> p d t"))
-        nc.sync.dma_start(out=pos_t[0][:], in_=pos1)
-        nc.sync.dma_start(out=w_raw23[:], in_=w_rows[:, :, 2 * P : H])
-        nc.sync.dma_start(out=pos_t[1][:], in_=pos2)
-        nc.sync.dma_start(out=pos_t[2][:], in_=pos3)
+        for d, pos in enumerate((pos1, pos2, pos3)):
+            nc.sync.dma_start(out=pos_t[d][:], in_=pos)
+        load_w(2)
+        load_w(3)
         load_words(nc, v_table, v_words)
 
         nc.scalar.activation(out=warm[:, 1:2], in_=warm[:, 0:1], func=SIGMOID)
 
-        def cast_w(m, raw, after=None):
+        def cast_w(m, after=None):
             grouped = sbuf(f"w_grouped{m}", [P, P, PACK], BF16, after)
-            nc.scalar.copy(out=grouped[:], in_=raw.rearrange("p j c -> p c j"))
+            nc.scalar.copy(out=grouped[:], in_=w_raw[m][:].rearrange("p j c -> p c j"))
             return grouped
 
         h = [sbuf(f"h{m}", [P, S], F32) for m in range(ROW_TILES)]
+        x_plane = sbuf("x_plane", [P, S], U8)
+        nc.vector.tensor_copy(out=x_plane[:], in_=x_table_plane[:].indirect(offs_t[:]))
         x_codes = sbuf("x_codes", [P, S], U32)
         nc.vector.tensor_copy(out=x_codes[:], in_=x_table[:].indirect(offs_t[:]))
-        x_planes = [sbuf("x_plane0", [P, HALF], U8), sbuf("x_plane1", [P, HALF], U8, "w_raw0")]
-        nc.vector.tensor_copy(out=x_planes[0][:], in_=x_table_plane[:].indirect(entries(offs_t, HALVES[0])))
-        w0 = quantise("w0", cast_w(0, w_raw0[:]))
-        nc.vector.tensor_copy(out=x_planes[1][:], in_=x_table_plane[:].indirect(entries(offs_t, HALVES[1])))
+        grouped0 = sbuf("w_grouped0", [P, P, PACK], BF16)
+        raw0 = w_raw[0][:].rearrange("p j c -> p c j")
+        nc.scalar.copy(out=grouped0[:, 0 : P // 2, :], in_=raw0[:, 0 : P // 2, :])
+        nc.gpsimd.tensor_scalar(
+            out=grouped0[:, P // 2 : P, :], in0=raw0[:, P // 2 : P, :], scalar1=1.0, scalar2=0.0, op0=MULT, op1=ADD
+        )
+        w0 = quantise("w0", grouped0)
         for a, cols in enumerate(HALVES):
             h_ps = bank(a, [P, HALF], f"h_ps0_{a}")
-            product(h_ps[:], *w0, x_codes[:, cols], x_planes[a][:])
+            product(h_ps[:], *w0, x_codes[:, cols], x_plane[:, cols])
             nc.scalar.copy(out=h[0][:, cols], in_=h_ps[:])
 
         def project(m, number, grouped):
             w_m = quantise(f"w{m}", grouped)
             h_ps = bank(number, [P, S], f"h_ps{m}")
-            for a, cols in enumerate(HALVES):
-                product(h_ps[:, cols], *w_m, x_codes[:, cols], x_planes[a][:])
-            return h_ps
+            product(h_ps[:], *w_m, x_codes[:], x_plane[:])
+            nc.scalar.copy(out=h[m][:], in_=h_ps[:])
 
-        zt = [sbuf(f"zt{b}", [P, 2, P, 2], BF16) for b in range(V // P)]
+        v_plane = sbuf("v_plane", [P, R], U8, "w_raw0")
+        nc.vector.tensor_copy(out=v_plane[:], in_=v_table_plane[:].indirect(cand_t[:]))
+        grouped1 = sbuf("w_grouped1", [P, P, PACK], BF16)
+        nc.gpsimd.tensor_scalar(
+            out=grouped1[:], in0=w_raw[1][:].rearrange("p j c -> p c j"), scalar1=1.0, scalar2=0.0, op0=MULT, op1=ADD
+        )
 
-        def windows(m, blocks, number, terms, before_last=None):
+        terms = {}
+
+        def windows(m, blocks, number, ahead=()):
             n = len(blocks)
             zt_ps = bank(number, [P, n, P], f"zt_ps{m}_{blocks[0]}")
             cols = slice(blocks[0] * P, (blocks[-1] + 1) * P)
             for d in range(D):
-                if d == D - 1 and before_last is not None:
-                    before_last()
+                after = None
+                if d in ahead:
+                    later, later_bank, grouped = ahead[d]
+                    project(later, later_bank, grouped)
+                    after = f"w_raw{later}"
+                term = sbuf(f"term{m}_{blocks[0]}_{d}", [P, n * P], F32, after)
+                terms[m, blocks[0], d] = term
                 nc.vector.tensor_tensor(
-                    out=terms[d], in0=h[m][:].indirect(entries(pos_t[d], cols)), in1=gate_t[:, d, cols], op=MULT
+                    out=term[:], in0=h[m][:].indirect(entries(pos_t[d], cols)), in1=gate_t[:, d, cols], op=MULT
                 )
                 for a in range(n):
                     nc.tensor.matmul(
                         out=zt_ps[:, a, :],
-                        lhsT=terms[d][:, a * P : (a + 1) * P],
+                        lhsT=term[:, a * P : (a + 1) * P],
                         rhs=ident[:],
                         is_transpose=True,
                         start=(d == 0 and a == 0),
                         stop=(d == D - 1 and a == n - 1),
                     )
+            return m, blocks, zt_ps
+
+        def round_z(m, blocks, zt_ps):
             words_here = slice(m * P // PACK, (m + 1) * P // PACK)
-            for a in range(n):
+            for a in range(len(blocks)):
                 nc.scalar.copy(
                     out=zt[blocks[a]][:, :, words_here, :],
                     in_=zt_ps[:, a, :].rearrange("t (p u e) -> t u p e", u=2, e=2),
@@ -172,44 +201,33 @@ def tile_picked_zcbow_sig_p_kernel(
             nc.scalar.copy(out=grouped_pairs, in_=z_ps[:].rearrange("p u t -> p t u"))
             return grouped
 
-        v_plane = sbuf("v_plane", [P, R], U8, "w_grouped0")
-        nc.vector.tensor_copy(out=v_plane[:], in_=v_table_plane[:].indirect(cand_t[:]))
-
-        h_ps1 = project(1, 3, cast_w(1, w_raw1[:]))
-        grouped2 = cast_w(2, w_raw23[:, :, 0:P], "w0_codes")
-        grouped3 = cast_w(3, w_raw23[:, :, P : 2 * P], "w0_plane")
-        nc.scalar.copy(out=h[1][:], in_=h_ps1[:])
-
-        def project_rest():
-            nc.scalar.copy(out=h[2][:], in_=project(2, 0, grouped2)[:])
-            nc.scalar.copy(out=h[3][:], in_=project(3, 1, grouped3)[:])
-
-        first_terms = [sbuf(f"term0_{d}", [P, V], F32, "w_raw23" if d == D - 1 else None)[:] for d in range(D)]
-        windows(0, [0, 1], 4, first_terms, project_rest)
-
-        for m in range(1, ROW_TILES):
-            windows(m, [0], 4 + m, [sbuf(f"term{m}_{d}", [P, P], F32)[:] for d in range(D)])
-        late = sbuf("late_terms", [P, (ROW_TILES - 1) * D, P], F32, f"term{ROW_TILES - 1}_0")
-        windows(1, [1], 2, [late[:, d, :] for d in range(D)])
+        sums0 = windows(0, [0, 1], 4, {0: (1, 2, grouped1)})
+        grouped2 = cast_w(2, "w1_codes")
+        grouped3 = cast_w(3, "w1_plane")
+        sums1 = windows(1, [0, 1], 5, {0: (2, 3, grouped2), 2: (3, 0, grouped3)})
+        zt = [sbuf(f"zt{b}", [P, 2, P, 2], BF16, ("w3_codes", "w3_plane")[b]) for b in range(V // P)]
+        round_z(*sums0)
+        round_z(*sums1)
+        round_z(*windows(2, [0, 1], 6))
+        round_z(*windows(3, [0], 7))
+        round_z(*windows(3, [1], 4))
         z_grouped0 = turn_z(0, 5)
-        windows(2, [1], 3, [late[:, D + d, :] for d in range(D)])
-        windows(3, [1], 4, [late[:, 2 * D + d, :] for d in range(D)])
-        z = [quantise("z0", z_grouped0)]
-
-        v_codes = sbuf("v_codes", [P, R], U32, "z_grouped0")
         z_grouped1 = turn_z(1, 6)
 
-        def score(b, cols, number, queue, after=None):
-            y_ps = bank(number, [P, HALF], f"y_ps{b}_{cols.start}")
-            product(y_ps[:], *z[b], v_codes[:, cols], v_plane[:, cols])
-            result = sbuf(f"result{b}_{cols.start}", [P, HALF], F32, after)
+        def score(b, a, number, queue, after=None):
+            cols = HALVES[a]
+            y_ps = bank(number, [P, HALF], f"y_ps{b}_{a}")
+            product(y_ps[:], *z[b], v_codes[a][:], v_plane[:, cols])
+            result = sbuf(f"result{b}_{a}", [P, HALF], F32, after)
             nc.scalar.activation(out=result[:], in_=y_ps[:], func=SIGMOID)
             queue.dma_start(out=out[b * P : (b + 1) * P, cols], in_=result[:])
 
-        nc.vector.tensor_copy(out=v_codes[:, HALVES[0]], in_=v_table[:].indirect(entries(cand_t, HALVES[0])))
-        score(0, HALVES[0], 4, nc.sync, "zt1")
-        nc.vector.tensor_copy(out=v_codes[:, HALVES[1]], in_=v_table[:].indirect(entries(cand_t, HALVES[1])))
-        score(0, HALVES[1], 0, nc.sync)
+        v_codes = [sbuf("v_codes0", [P, HALF], U32, "term3_1_0"), sbuf("v_codes1", [P, HALF], U32, "z_grouped0")]
+        nc.vector.tensor_copy(out=v_codes[0][:], in_=v_table[:].indirect(entries(cand_t, HALVES[0])))
+        z = [quantise("z0", z_grouped0)]
+        score(0, 0, 4, nc.sync, "w3_plane")
+        nc.vector.tensor_copy(out=v_codes[1][:], in_=v_table[:].indirect(entries(cand_t, HALVES[1])))
         z.append(quantise("z1", z_grouped1))
-        score(1, HALVES[0], 1, nc.sync)
-        score(1, HALVES[1], 2, nc.scalar)
+        score(0, 1, 2, nc.sync)
+        score(1, 0, 3, nc.sync)
+        score(1, 1, 0, nc.scalar)

@@ -14,7 +14,6 @@ U16 = mybir.dt.uint16
 U8 = mybir.dt.uint8
 FP8X4 = mybir.dt.float8_e4m3fn_x4
 MULT = mybir.AluOpType.mult
-ADD = mybir.AluOpType.add
 SIGMOID = mybir.ActivationFunctionType.Sigmoid
 
 P = 128
@@ -35,14 +34,6 @@ def load_scale_rows(nc, plane, scales):
         nc.sync.dma_start(
             out=plane[QUADRANT * q : QUADRANT * q + PACK, :].bitcast(I32),
             in_=scales[0, PACK * q : PACK * (q + 1), :].bitcast(I32),
-        )
-
-
-def load_scale_rows_repeated(nc, plane, scales):
-    for q in range(P // QUADRANT):
-        nc.sync.dma_start(
-            out=plane[QUADRANT * q : QUADRANT * (q + 1), :].bitcast(I32),
-            in_=scales[0, PACK * q : PACK * (q + 1), :].bitcast(I32).partition_broadcast(QUADRANT // PACK),
         )
 
 
@@ -91,82 +82,69 @@ def tile_picked_zcbow_sig_p_kernel(
         v_table = sbuf("v_table", [P, G], U32)
         v_table_plane = sbuf("v_table_plane", [P, G], U8)
         gate_t = sbuf("gate_t", [P, D, V], F32)
-        w_raw = [sbuf(f"w_raw{m}", [P, PACK, P], F32) for m in range(ROW_TILES)]
+        w_raw23 = sbuf("w_raw23", [P, PACK, 2 * P], F32)
+        w_raw = [sbuf(f"w_raw{m}", [P, PACK, P], F32)[:] for m in range(2)]
+        w_raw.extend([w_raw23[:, :, 0:P], w_raw23[:, :, P : 2 * P]])
         ident = sbuf("ident", [P, P], F32)
         warm = sbuf("warm", [P, 8], F32)
 
+        nc.vector.memset(x_table_plane[:].bitcast(I32), 0)
         nc.vector.memset(v_table_plane[:].bitcast(I32), 0)
         nc.gpsimd.memset(warm[:], 0.0)
         make_identity(nc, ident[:])
 
         w_rows = w1.rearrange("(p j) c -> p j c", j=PACK)
-
-        def load_w(m):
-            nc.sync.dma_start(out=w_raw[m][:], in_=w_rows[:, :, m * P : (m + 1) * P])
-
         nc.sync.dma_start(out=offs_t[:], in_=offs)
-        load_scale_rows_repeated(nc, x_table_plane, x_scales)
-        nc.sync.dma_start(out=cand_t[:], in_=cand)
         load_words(nc, x_table, x_words)
-        load_w(0)
+        load_scale_rows(nc, x_table_plane, x_scales)
+        nc.sync.dma_start(out=w_raw[0], in_=w_rows[:, :, 0:P])
+        nc.sync.dma_start(out=cand_t[:], in_=cand)
+        nc.sync.dma_start(out=w_raw[1], in_=w_rows[:, :, P : 2 * P])
         load_scale_rows(nc, v_table_plane, v_scales)
-        load_w(1)
         nc.sync.dma_start(out=gate_t[:], in_=gate.rearrange("d p t -> p d t"))
-        for d, pos in enumerate((pos1, pos2, pos3)):
-            nc.sync.dma_start(out=pos_t[d][:], in_=pos)
-        load_w(2)
-        load_w(3)
+        nc.sync.dma_start(out=pos_t[0][:], in_=pos1)
+        nc.sync.dma_start(out=w_raw23[:], in_=w_rows[:, :, 2 * P : H])
+        nc.sync.dma_start(out=pos_t[1][:], in_=pos2)
+        nc.sync.dma_start(out=pos_t[2][:], in_=pos3)
         load_words(nc, v_table, v_words)
 
         nc.scalar.activation(out=warm[:, 1:2], in_=warm[:, 0:1], func=SIGMOID)
 
         def cast_w(m, after=None):
             grouped = sbuf(f"w_grouped{m}", [P, P, PACK], BF16, after)
-            nc.scalar.copy(out=grouped[:], in_=w_raw[m][:].rearrange("p j c -> p c j"))
+            nc.scalar.copy(out=grouped[:], in_=w_raw[m].rearrange("p j c -> p c j"))
             return grouped
 
         h = [sbuf(f"h{m}", [P, S], F32) for m in range(ROW_TILES)]
-        x_plane = sbuf("x_plane", [P, S], U8)
-        nc.vector.tensor_copy(out=x_plane[:], in_=x_table_plane[:].indirect(offs_t[:]))
         x_codes = sbuf("x_codes", [P, S], U32)
         nc.vector.tensor_copy(out=x_codes[:], in_=x_table[:].indirect(offs_t[:]))
-        grouped0 = sbuf("w_grouped0", [P, P, PACK], BF16)
-        raw0 = w_raw[0][:].rearrange("p j c -> p c j")
-        nc.scalar.copy(out=grouped0[:, 0 : P // 2, :], in_=raw0[:, 0 : P // 2, :])
-        nc.gpsimd.tensor_scalar(
-            out=grouped0[:, P // 2 : P, :], in0=raw0[:, P // 2 : P, :], scalar1=1.0, scalar2=0.0, op0=MULT, op1=ADD
-        )
-        w0 = quantise("w0", grouped0)
+        x_planes = [sbuf("x_plane0", [P, HALF], U8), sbuf("x_plane1", [P, HALF], U8, "w_raw0")]
+        nc.vector.tensor_copy(out=x_planes[0][:], in_=x_table_plane[:].indirect(entries(offs_t, HALVES[0])))
+        w0 = quantise("w0", cast_w(0))
+        nc.vector.tensor_copy(out=x_planes[1][:], in_=x_table_plane[:].indirect(entries(offs_t, HALVES[1])))
         for a, cols in enumerate(HALVES):
             h_ps = bank(a, [P, HALF], f"h_ps0_{a}")
-            product(h_ps[:], *w0, x_codes[:, cols], x_plane[:, cols])
+            product(h_ps[:], *w0, x_codes[:, cols], x_planes[a][:])
             nc.scalar.copy(out=h[0][:, cols], in_=h_ps[:])
 
         def project(m, number, grouped):
             w_m = quantise(f"w{m}", grouped)
             h_ps = bank(number, [P, S], f"h_ps{m}")
-            product(h_ps[:], *w_m, x_codes[:], x_plane[:])
+            for a, cols in enumerate(HALVES):
+                product(h_ps[:, cols], *w_m, x_codes[:, cols], x_planes[a][:])
             nc.scalar.copy(out=h[m][:], in_=h_ps[:])
 
-        v_plane = sbuf("v_plane", [P, R], U8, "w_raw0")
+        v_plane = sbuf("v_plane", [P, R], U8, "w_grouped0")
         nc.vector.tensor_copy(out=v_plane[:], in_=v_table_plane[:].indirect(cand_t[:]))
-        grouped1 = sbuf("w_grouped1", [P, P, PACK], BF16)
-        nc.gpsimd.tensor_scalar(
-            out=grouped1[:], in0=w_raw[1][:].rearrange("p j c -> p c j"), scalar1=1.0, scalar2=0.0, op0=MULT, op1=ADD
-        )
 
         terms = {}
 
-        def windows(m, blocks, number, ahead=()):
+        def windows(m, blocks, number, ahead={}):
             n = len(blocks)
             zt_ps = bank(number, [P, n, P], f"zt_ps{m}_{blocks[0]}")
             cols = slice(blocks[0] * P, (blocks[-1] + 1) * P)
             for d in range(D):
-                after = None
-                if d in ahead:
-                    later, later_bank, grouped = ahead[d]
-                    project(later, later_bank, grouped)
-                    after = f"w_raw{later}"
+                after = ahead.get(d)
                 term = sbuf(f"term{m}_{blocks[0]}_{d}", [P, n * P], F32, after)
                 terms[m, blocks[0], d] = term
                 nc.vector.tensor_tensor(
@@ -201,14 +179,15 @@ def tile_picked_zcbow_sig_p_kernel(
             nc.scalar.copy(out=grouped_pairs, in_=z_ps[:].rearrange("p u t -> p t u"))
             return grouped
 
-        sums0 = windows(0, [0, 1], 4, {0: (1, 2, grouped1)})
-        grouped2 = cast_w(2, "w1_codes")
-        grouped3 = cast_w(3, "w1_plane")
-        sums1 = windows(1, [0, 1], 5, {0: (2, 3, grouped2), 2: (3, 0, grouped3)})
-        zt = [sbuf(f"zt{b}", [P, 2, P, 2], BF16, ("w3_codes", "w3_plane")[b]) for b in range(V // P)]
+        project(1, 2, cast_w(1))
+        sums0 = windows(0, [0, 1], 2)
+        project(2, 3, cast_w(2, "w1_codes"))
+        project(3, 0, cast_w(3, "term0_0_0"))
+        sums1 = windows(1, [0, 1], 3, {1: "w1_codes"})
+        zt = [sbuf(f"zt{b}", [P, 2, P, 2], BF16, ("term1_0_0", "term1_0_2")[b]) for b in range(V // P)]
         round_z(*sums0)
         round_z(*sums1)
-        round_z(*windows(2, [0, 1], 6))
+        round_z(*windows(2, [0, 1], 0))
         round_z(*windows(3, [0], 7))
         round_z(*windows(3, [1], 4))
         z_grouped0 = turn_z(0, 5)
@@ -225,9 +204,9 @@ def tile_picked_zcbow_sig_p_kernel(
         v_codes = [sbuf("v_codes0", [P, HALF], U32, "term3_1_0"), sbuf("v_codes1", [P, HALF], U32, "z_grouped0")]
         nc.vector.tensor_copy(out=v_codes[0][:], in_=v_table[:].indirect(entries(cand_t, HALVES[0])))
         z = [quantise("z0", z_grouped0)]
-        score(0, 0, 4, nc.sync, "w3_plane")
+        score(0, 0, 4, nc.sync, "term1_0_2")
         nc.vector.tensor_copy(out=v_codes[1][:], in_=v_table[:].indirect(entries(cand_t, HALVES[1])))
         z.append(quantise("z1", z_grouped1))
         score(0, 1, 2, nc.sync)
         score(1, 0, 3, nc.sync)
-        score(1, 1, 0, nc.scalar)
+        score(1, 1, 1, nc.scalar)

@@ -209,4 +209,4 @@ def tile_picked_zcbow_sig_p_kernel(
         z.append(quantise("z1", z_grouped1))
         score(0, 1, 2, nc.sync)
         score(1, 0, 3, nc.sync)
-        score(1, 1, 1, nc.scalar)
+        score(1, 1, 1, nc.sync)

@@ -21,6 +21,7 @@ PACK = 4
 QUADRANT = 32
 LIST_ROWS = 16
 ROW_TILES = H // P
+SCALE_ROWS = 16
 HALF = 256
 HALVES = (slice(0, HALF), slice(HALF, 2 * HALF))
 
@@ -29,12 +30,9 @@ def load_words(nc, tile, words):
     nc.sync.dma_start(out=tile[:].bitcast(I32), in_=words[0].rearrange("p n t -> p (n t)").bitcast(I32))
 
 
-def load_scale_rows(nc, plane, scales):
-    for q in range(P // QUADRANT):
-        nc.sync.dma_start(
-            out=plane[QUADRANT * q : QUADRANT * q + PACK, :].bitcast(I32),
-            in_=scales[0, PACK * q : PACK * (q + 1), :].bitcast(I32),
-        )
+def load_scale_rows(queue, plane, scales):
+    for r in range(PACK):
+        queue.dma_start(out=plane[r:P:QUADRANT, :].bitcast(I32), in_=scales[r:SCALE_ROWS:PACK, :].bitcast(I32))
 
 
 def entries(offsets, cols):
@@ -66,12 +64,15 @@ def tile_picked_zcbow_sig_p_kernel(
                 stop=True,
             )
 
+        made = {}
+
         def quantise(name, grouped):
             codes = sbuf(f"{name}_codes", [P, P], U32)
             plane = sbuf(f"{name}_plane", [P, P], U8)
             nc.vector.quantize_mx(
                 out=codes[:].bitcast(FP8X4), scales=plane[:], in_=grouped[:].rearrange("p c j -> p (c j)")
             )
+            made[name] = codes
             return codes[:], plane[:]
 
         offs_t = sbuf("offs_t", [P, S // LIST_ROWS], U16)
@@ -82,30 +83,28 @@ def tile_picked_zcbow_sig_p_kernel(
         v_table = sbuf("v_table", [P, G], U32)
         v_table_plane = sbuf("v_table_plane", [P, G], U8)
         gate_t = sbuf("gate_t", [P, D, V], F32)
-        w_raw23 = sbuf("w_raw23", [P, PACK, 2 * P], F32)
-        w_raw = [sbuf(f"w_raw{m}", [P, PACK, P], F32)[:] for m in range(2)]
-        w_raw.extend([w_raw23[:, :, 0:P], w_raw23[:, :, P : 2 * P]])
+        w_raw = [sbuf(f"w_raw{m}", [P, PACK, P], F32)[:] for m in range(ROW_TILES)]
         ident = sbuf("ident", [P, P], F32)
         warm = sbuf("warm", [P, 8], F32)
 
         nc.vector.memset(x_table_plane[:].bitcast(I32), 0)
-        nc.vector.memset(v_table_plane[:].bitcast(I32), 0)
         nc.gpsimd.memset(warm[:], 0.0)
+        nc.gpsimd.memset(v_table_plane[:].bitcast(I32), 0)
+        nc.gpsimd.dma_start(out=v_table_plane[0:SCALE_ROWS, :].bitcast(I32), in_=v_scales[0].bitcast(I32))
         make_identity(nc, ident[:])
 
         w_rows = w1.rearrange("(p j) c -> p j c", j=PACK)
         nc.sync.dma_start(out=offs_t[:], in_=offs)
         load_words(nc, x_table, x_words)
-        load_scale_rows(nc, x_table_plane, x_scales)
+        load_scale_rows(nc.sync, x_table_plane, x_scales[0])
         nc.sync.dma_start(out=w_raw[0], in_=w_rows[:, :, 0:P])
         nc.sync.dma_start(out=cand_t[:], in_=cand)
         nc.sync.dma_start(out=w_raw[1], in_=w_rows[:, :, P : 2 * P])
-        load_scale_rows(nc, v_table_plane, v_scales)
         nc.sync.dma_start(out=gate_t[:], in_=gate.rearrange("d p t -> p d t"))
-        nc.sync.dma_start(out=pos_t[0][:], in_=pos1)
-        nc.sync.dma_start(out=w_raw23[:], in_=w_rows[:, :, 2 * P : H])
-        nc.sync.dma_start(out=pos_t[1][:], in_=pos2)
-        nc.sync.dma_start(out=pos_t[2][:], in_=pos3)
+        for d, pos in enumerate((pos1, pos2, pos3)):
+            nc.sync.dma_start(out=pos_t[d][:], in_=pos)
+        for m in range(2, ROW_TILES):
+            nc.sync.dma_start(out=w_raw[m], in_=w_rows[:, :, m * P : (m + 1) * P])
         load_words(nc, v_table, v_words)
 
         nc.scalar.activation(out=warm[:, 1:2], in_=warm[:, 0:1], func=SIGMOID)
@@ -118,48 +117,56 @@ def tile_picked_zcbow_sig_p_kernel(
         h = [sbuf(f"h{m}", [P, S], F32) for m in range(ROW_TILES)]
         x_codes = sbuf("x_codes", [P, S], U32)
         nc.vector.tensor_copy(out=x_codes[:], in_=x_table[:].indirect(offs_t[:]))
-        x_planes = [sbuf("x_plane0", [P, HALF], U8), sbuf("x_plane1", [P, HALF], U8, "w_raw0")]
-        nc.vector.tensor_copy(out=x_planes[0][:], in_=x_table_plane[:].indirect(entries(offs_t, HALVES[0])))
+        x_plane = sbuf("x_plane", [P, S], U8)
+        nc.vector.tensor_copy(out=x_plane[:], in_=x_table_plane[:].indirect(offs_t[:]))
         w0 = quantise("w0", cast_w(0))
-        nc.vector.tensor_copy(out=x_planes[1][:], in_=x_table_plane[:].indirect(entries(offs_t, HALVES[1])))
+        grouped1 = cast_w(1)
         for a, cols in enumerate(HALVES):
             h_ps = bank(a, [P, HALF], f"h_ps0_{a}")
-            product(h_ps[:], *w0, x_codes[:, cols], x_planes[a][:])
+            product(h_ps[:], *w0, x_codes[:, cols], x_plane[:, cols])
             nc.scalar.copy(out=h[0][:, cols], in_=h_ps[:])
 
         def project(m, number, grouped):
             w_m = quantise(f"w{m}", grouped)
             h_ps = bank(number, [P, S], f"h_ps{m}")
-            for a, cols in enumerate(HALVES):
-                product(h_ps[:, cols], *w_m, x_codes[:, cols], x_planes[a][:])
+            product(h_ps[:], *w_m, x_codes[:], x_plane[:])
             nc.scalar.copy(out=h[m][:], in_=h_ps[:])
 
-        v_plane = sbuf("v_plane", [P, R], U8, "w_grouped0")
-        nc.vector.tensor_copy(out=v_plane[:], in_=v_table_plane[:].indirect(cand_t[:]))
+        v_rows = [sbuf("v_rows0", [P, HALF], U8, "w_raw0"), sbuf("v_rows1", [P, HALF], U8, "w_raw1")]
+        nc.vector.tensor_copy(out=v_rows[0][:], in_=v_table_plane[:].indirect(entries(cand_t, HALVES[0])))
+        project(1, 2, grouped1)
+        nc.vector.tensor_copy(out=v_rows[1][:], in_=v_table_plane[:].indirect(entries(cand_t, HALVES[1])))
 
         terms = {}
 
-        def windows(m, blocks, number, ahead={}):
+        def sums(m, blocks, number):
+            return m, blocks, bank(number, [P, len(blocks), P], f"zt_ps{m}_{blocks[0]}")
+
+        def term(group, d, after=None, part=None):
+            m, blocks, zt_ps = group
             n = len(blocks)
-            zt_ps = bank(number, [P, n, P], f"zt_ps{m}_{blocks[0]}")
             cols = slice(blocks[0] * P, (blocks[-1] + 1) * P)
-            for d in range(D):
-                after = ahead.get(d)
-                term = sbuf(f"term{m}_{blocks[0]}_{d}", [P, n * P], F32, after)
-                terms[m, blocks[0], d] = term
-                nc.vector.tensor_tensor(
-                    out=term[:], in0=h[m][:].indirect(entries(pos_t[d], cols)), in1=gate_t[:, d, cols], op=MULT
+            if part is None:
+                part = sbuf(f"term{m}_{blocks[0]}_{d}", [P, n * P], F32, after)
+            terms[m, blocks[0], d] = part
+            nc.vector.tensor_tensor(
+                out=part[:], in0=h[m][:].indirect(entries(pos_t[d], cols)), in1=gate_t[:, d, cols], op=MULT
+            )
+            for a in range(n):
+                nc.tensor.matmul(
+                    out=zt_ps[:, a, :],
+                    lhsT=part[:, a * P : (a + 1) * P],
+                    rhs=ident[:],
+                    is_transpose=True,
+                    start=(d == 0 and a == 0),
+                    stop=(d == D - 1 and a == n - 1),
                 )
-                for a in range(n):
-                    nc.tensor.matmul(
-                        out=zt_ps[:, a, :],
-                        lhsT=term[:, a * P : (a + 1) * P],
-                        rhs=ident[:],
-                        is_transpose=True,
-                        start=(d == 0 and a == 0),
-                        stop=(d == D - 1 and a == n - 1),
-                    )
-            return m, blocks, zt_ps
+
+        def windows(m, blocks, number):
+            group = sums(m, blocks, number)
+            for d in range(D):
+                term(group, d)
+            return group
 
         def round_z(m, blocks, zt_ps):
             words_here = slice(m * P // PACK, (m + 1) * P // PACK)
@@ -179,19 +186,25 @@ def tile_picked_zcbow_sig_p_kernel(
             nc.scalar.copy(out=grouped_pairs, in_=z_ps[:].rearrange("p u t -> p t u"))
             return grouped
 
-        project(1, 2, cast_w(1))
-        sums0 = windows(0, [0, 1], 2)
-        project(2, 3, cast_w(2, "w1_codes"))
-        project(3, 0, cast_w(3, "term0_0_0"))
-        sums1 = windows(1, [0, 1], 3, {1: "w1_codes"})
-        zt = [sbuf(f"zt{b}", [P, 2, P, 2], BF16, ("term1_0_0", "term1_0_2")[b]) for b in range(V // P)]
+        sums0 = windows(0, [0, 1], 3)
+        project(2, 0, cast_w(2))
+        v_plane = sbuf("v_plane", [P, R], U8, "w_grouped2")
+        for a, cols in enumerate(HALVES):
+            load_scale_rows(nc.sync, v_plane[:, cols], v_rows[a])
+        sums1 = sums(1, [0, 1], 2)
+        pair = sbuf("term1_pair", [P, 2 * V], F32, "w_raw2")
+        term(sums1, 0, part=pair[:, 0:V])
+        term(sums1, 1, part=pair[:, V : 2 * V])
+        project(3, 1, cast_w(3))
+        term(sums1, 2, "w_raw3")
+        zt = [sbuf(f"zt{b}", [P, 2, P, 2], BF16, ("w_grouped3", "w3_codes")[b]) for b in range(V // P)]
         round_z(*sums0)
         round_z(*sums1)
-        round_z(*windows(2, [0, 1], 0))
-        round_z(*windows(3, [0], 7))
-        round_z(*windows(3, [1], 4))
-        z_grouped0 = turn_z(0, 5)
-        z_grouped1 = turn_z(1, 6)
+        round_z(*windows(2, [0, 1], 4))
+        round_z(*windows(3, [0], 5))
+        round_z(*windows(3, [1], 6))
+        z_grouped0 = turn_z(0, 7)
+        z_grouped1 = turn_z(1, 0)
 
         def score(b, a, number, queue, after=None):
             cols = HALVES[a]
@@ -204,9 +217,9 @@ def tile_picked_zcbow_sig_p_kernel(
         v_codes = [sbuf("v_codes0", [P, HALF], U32, "term3_1_0"), sbuf("v_codes1", [P, HALF], U32, "z_grouped0")]
         nc.vector.tensor_copy(out=v_codes[0][:], in_=v_table[:].indirect(entries(cand_t, HALVES[0])))
         z = [quantise("z0", z_grouped0)]
-        score(0, 0, 4, nc.sync, "term1_0_2")
+        score(0, 0, 1, nc.sync, "w3_codes")
         nc.vector.tensor_copy(out=v_codes[1][:], in_=v_table[:].indirect(entries(cand_t, HALVES[1])))
         z.append(quantise("z1", z_grouped1))
         score(0, 1, 2, nc.sync)
         score(1, 0, 3, nc.sync)
-        score(1, 1, 1, nc.sync)
+        score(1, 1, 4, nc.sync)

@@ -45,10 +45,14 @@ def tile_picked_zcbow_sig_p_kernel(
     nc = tc.nc
     with ExitStack() as ctx:
         keep = ctx.enter_context(tc.tile_pool(name="keep", bufs=1))
+        shared = ctx.enter_context(tc.tile_pool(name="shared", bufs=1))
         psum = ctx.enter_context(tc.psum_pool(name="psum", bufs=1))
 
         def sbuf(name, shape, dtype, after=None):
             return keep.tile(shape, dtype, name=name, tag=after or name, align_bytes=64)
+
+        def placed(name, shape, offset):
+            return shared.tile(shape, F32, name=name, offset=offset, align_bytes=64)
 
         def bank(number, shape, name):
             return psum.tile(shape, F32, name=name, tag=f"bank{number}")
@@ -83,14 +87,15 @@ def tile_picked_zcbow_sig_p_kernel(
         v_table = sbuf("v_table", [P, G], U32)
         v_table_plane = sbuf("v_table_plane", [P, G], U8)
         gate_t = sbuf("gate_t", [P, D, V], F32)
-        w_raw = [sbuf(f"w_raw{m}", [P, PACK, P], F32)[:] for m in range(ROW_TILES)]
+        w_raw = [sbuf(f"w_raw{m}", [P, PACK, P], F32)[:] for m in range(2)]
+        w_raw.append(placed("w_raw2", [P, PACK, P], 0)[:])
+        w_raw.append(sbuf("w_raw3", [P, PACK, P], F32)[:])
         ident = sbuf("ident", [P, P], F32)
         warm = sbuf("warm", [P, 8], F32)
 
         nc.vector.memset(x_table_plane[:].bitcast(I32), 0)
+        nc.vector.memset(v_table_plane[:].bitcast(I32), 0)
         nc.gpsimd.memset(warm[:], 0.0)
-        nc.gpsimd.memset(v_table_plane[:].bitcast(I32), 0)
-        nc.gpsimd.dma_start(out=v_table_plane[0:SCALE_ROWS, :].bitcast(I32), in_=v_scales[0].bitcast(I32))
         make_identity(nc, ident[:])
 
         w_rows = w1.rearrange("(p j) c -> p j c", j=PACK)
@@ -98,44 +103,49 @@ def tile_picked_zcbow_sig_p_kernel(
         load_words(nc, x_table, x_words)
         load_scale_rows(nc.sync, x_table_plane, x_scales[0])
         nc.sync.dma_start(out=w_raw[0], in_=w_rows[:, :, 0:P])
-        nc.sync.dma_start(out=cand_t[:], in_=cand)
         nc.sync.dma_start(out=w_raw[1], in_=w_rows[:, :, P : 2 * P])
         nc.sync.dma_start(out=gate_t[:], in_=gate.rearrange("d p t -> p d t"))
         for d, pos in enumerate((pos1, pos2, pos3)):
             nc.sync.dma_start(out=pos_t[d][:], in_=pos)
         for m in range(2, ROW_TILES):
             nc.sync.dma_start(out=w_raw[m], in_=w_rows[:, :, m * P : (m + 1) * P])
+        nc.sync.dma_start(out=cand_t[:], in_=cand)
+        load_scale_rows(nc.sync, v_table_plane, v_scales[0])
         load_words(nc, v_table, v_words)
 
         nc.scalar.activation(out=warm[:, 1:2], in_=warm[:, 0:1], func=SIGMOID)
 
         def cast_w(m, after=None):
             grouped = sbuf(f"w_grouped{m}", [P, P, PACK], BF16, after)
-            nc.scalar.copy(out=grouped[:], in_=w_raw[m].rearrange("p j c -> p c j"))
+            nc.scalar.copy(
+                out=grouped[:].rearrange("p (c i) j -> p c j i", i=PACK),
+                in_=w_raw[m].rearrange("p j (c i) -> p c j i", i=PACK),
+            )
             return grouped
 
-        h = [sbuf(f"h{m}", [P, S], F32) for m in range(ROW_TILES)]
+        h = {0: sbuf("h0", [P, S], F32)}
         x_codes = sbuf("x_codes", [P, S], U32)
         nc.vector.tensor_copy(out=x_codes[:], in_=x_table[:].indirect(offs_t[:]))
-        x_plane = sbuf("x_plane", [P, S], U8)
-        nc.vector.tensor_copy(out=x_plane[:], in_=x_table_plane[:].indirect(offs_t[:]))
+        early, late = slice(0, S - P), slice(S - P, S)
+        x_plane = sbuf("x_plane", [P, S - P], U8)
+        x_plane_late = sbuf("x_plane_late", [P, P], U8, "w_raw0")
+        nc.vector.tensor_copy(out=x_plane[:], in_=x_table_plane[:].indirect(entries(offs_t, early)))
         w0 = quantise("w0", cast_w(0))
+        nc.vector.tensor_copy(out=x_plane_late[:], in_=x_table_plane[:].indirect(entries(offs_t, late)))
         grouped1 = cast_w(1)
-        for a, cols in enumerate(HALVES):
-            h_ps = bank(a, [P, HALF], f"h_ps0_{a}")
-            product(h_ps[:], *w0, x_codes[:, cols], x_plane[:, cols])
-            nc.scalar.copy(out=h[0][:, cols], in_=h_ps[:])
 
-        def project(m, number, grouped):
-            w_m = quantise(f"w{m}", grouped)
-            h_ps = bank(number, [P, S], f"h_ps{m}")
-            product(h_ps[:], *w_m, x_codes[:], x_plane[:])
-            nc.scalar.copy(out=h[m][:], in_=h_ps[:])
+        def project(m, banks, grouped_or_codes):
+            for a, cols in enumerate(HALVES):
+                h_ps = bank(banks[a], [P, HALF], f"h_ps{m}_{a}")
+                if a == 0:
+                    product(h_ps[:], *grouped_or_codes, x_codes[:, cols], x_plane[:, cols])
+                else:
+                    product(h_ps[:, 0:P], *grouped_or_codes, x_codes[:, HALF : S - P], x_plane[:, HALF : S - P])
+                    product(h_ps[:, P:HALF], *grouped_or_codes, x_codes[:, late], x_plane_late[:])
+                nc.scalar.copy(out=h[m][:, cols], in_=h_ps[:])
 
-        v_rows = [sbuf("v_rows0", [P, HALF], U8, "w_raw0"), sbuf("v_rows1", [P, HALF], U8, "w_raw1")]
-        nc.vector.tensor_copy(out=v_rows[0][:], in_=v_table_plane[:].indirect(entries(cand_t, HALVES[0])))
-        project(1, 2, grouped1)
-        nc.vector.tensor_copy(out=v_rows[1][:], in_=v_table_plane[:].indirect(entries(cand_t, HALVES[1])))
+        project(0, (0, 1), w0)
+        codes1 = quantise("w1", grouped1)
 
         terms = {}
 
@@ -186,18 +196,23 @@ def tile_picked_zcbow_sig_p_kernel(
             nc.scalar.copy(out=grouped_pairs, in_=z_ps[:].rearrange("p u t -> p t u"))
             return grouped
 
-        sums0 = windows(0, [0, 1], 3)
-        project(2, 0, cast_w(2))
-        v_plane = sbuf("v_plane", [P, R], U8, "w_grouped2")
-        for a, cols in enumerate(HALVES):
-            load_scale_rows(nc.sync, v_plane[:, cols], v_rows[a])
+        sums0 = sums(0, [0, 1], 3)
+        term(sums0, 0)
+        term(sums0, 1)
+        grouped2 = cast_w(2)
+        h[1] = placed("h1", [P, S], 1024)
+        project(1, (2, 4), codes1)
+        h[2] = sbuf("h2", [P, S], F32)
+        project(2, (0, 1), quantise("w2", grouped2))
+        term(sums0, 2, part=placed("term0_2", [P, V], 0)[:])
         sums1 = sums(1, [0, 1], 2)
-        pair = sbuf("term1_pair", [P, 2 * V], F32, "w_raw2")
-        term(sums1, 0, part=pair[:, 0:V])
-        term(sums1, 1, part=pair[:, V : 2 * V])
-        project(3, 1, cast_w(3))
-        term(sums1, 2, "w_raw3")
-        zt = [sbuf(f"zt{b}", [P, 2, P, 2], BF16, ("w_grouped3", "w3_codes")[b]) for b in range(V // P)]
+        term(sums1, 0)
+        h[3] = sbuf("h3", [P, S], F32)
+        project(3, (5, 6), quantise("w3", cast_w(3, "w_grouped2")))
+        pair = sbuf("term1_pair", [P, 2 * V], F32, "w_raw3")
+        term(sums1, 1, part=pair[:, 0:V])
+        term(sums1, 2, part=pair[:, V : 2 * V])
+        zt = [sbuf(f"zt{b}", [P, 2, P, 2], BF16, ("w_grouped2", "w3_codes")[b]) for b in range(V // P)]
         round_z(*sums0)
         round_z(*sums1)
         round_z(*windows(2, [0, 1], 4))
@@ -216,6 +231,8 @@ def tile_picked_zcbow_sig_p_kernel(
 
         v_codes = [sbuf("v_codes0", [P, HALF], U32, "term3_1_0"), sbuf("v_codes1", [P, HALF], U32, "z_grouped0")]
         nc.vector.tensor_copy(out=v_codes[0][:], in_=v_table[:].indirect(entries(cand_t, HALVES[0])))
+        v_plane = sbuf("v_plane", [P, R], U8, "term3_0_2")
+        nc.vector.tensor_copy(out=v_plane[:], in_=v_table_plane[:].indirect(cand_t[:]))
         z = [quantise("z0", z_grouped0)]
         score(0, 0, 1, nc.sync, "w3_codes")
         nc.vector.tensor_copy(out=v_codes[1][:], in_=v_table[:].indirect(entries(cand_t, HALVES[1])))

@@ -51,8 +51,8 @@ def tile_picked_zcbow_sig_p_kernel(
         def sbuf(name, shape, dtype, after=None):
             return keep.tile(shape, dtype, name=name, tag=after or name, align_bytes=64)
 
-        def placed(name, shape, offset):
-            return shared.tile(shape, F32, name=name, offset=offset, align_bytes=64)
+        def placed(name, shape, offset, dtype=F32):
+            return shared.tile(shape, dtype, name=name, offset=offset, align_bytes=64)
 
         def bank(number, shape, name):
             return psum.tile(shape, F32, name=name, tag=f"bank{number}")
@@ -70,8 +70,11 @@ def tile_picked_zcbow_sig_p_kernel(
 
         made = {}
 
-        def quantise(name, grouped):
-            codes = sbuf(f"{name}_codes", [P, P], U32)
+        def quantise(name, grouped, offset=None):
+            if offset is None:
+                codes = sbuf(f"{name}_codes", [P, P], U32)
+            else:
+                codes = placed(f"{name}_codes", [P, P], offset, U32)
             plane = sbuf(f"{name}_plane", [P, P], U8)
             nc.vector.quantize_mx(
                 out=codes[:].bitcast(FP8X4), scales=plane[:], in_=grouped[:].rearrange("p c j -> p (c j)")
@@ -84,7 +87,7 @@ def tile_picked_zcbow_sig_p_kernel(
         pos_t = [sbuf(f"pos_t{d}", [P, V // LIST_ROWS], U16) for d in range(D)]
         x_table = sbuf("x_table", [P, T], U32)
         x_table_plane = sbuf("x_table_plane", [P, T], U8)
-        v_table = sbuf("v_table", [P, G], U32)
+        v_table = placed("v_table", [P, G], 8192, U32)
         v_table_plane = sbuf("v_table_plane", [P, G], U8)
         gate_t = sbuf("gate_t", [P, D, V], F32)
         w_raw = [sbuf(f"w_raw{m}", [P, PACK, P], F32)[:] for m in range(2)]
@@ -93,9 +96,10 @@ def tile_picked_zcbow_sig_p_kernel(
         ident = sbuf("ident", [P, P], F32)
         warm = sbuf("warm", [P, 8], F32)
 
-        nc.vector.memset(x_table_plane[:].bitcast(I32), 0)
-        nc.vector.memset(v_table_plane[:].bitcast(I32), 0)
+        nc.gpsimd.memset(x_table_plane[:].bitcast(I32), 0)
         nc.gpsimd.memset(warm[:], 0.0)
+        nc.gpsimd.memset(v_table_plane[:].bitcast(I32), 0)
+        nc.gpsimd.dma_start(out=v_table_plane[0:SCALE_ROWS, :].bitcast(I32), in_=v_scales[0].bitcast(I32))
         make_identity(nc, ident[:])
 
         w_rows = w1.rearrange("(p j) c -> p j c", j=PACK)
@@ -104,13 +108,12 @@ def tile_picked_zcbow_sig_p_kernel(
         load_scale_rows(nc.sync, x_table_plane, x_scales[0])
         nc.sync.dma_start(out=w_raw[0], in_=w_rows[:, :, 0:P])
         nc.sync.dma_start(out=w_raw[1], in_=w_rows[:, :, P : 2 * P])
+        nc.sync.dma_start(out=cand_t[:], in_=cand)
         nc.sync.dma_start(out=gate_t[:], in_=gate.rearrange("d p t -> p d t"))
         for d, pos in enumerate((pos1, pos2, pos3)):
             nc.sync.dma_start(out=pos_t[d][:], in_=pos)
         for m in range(2, ROW_TILES):
             nc.sync.dma_start(out=w_raw[m], in_=w_rows[:, :, m * P : (m + 1) * P])
-        nc.sync.dma_start(out=cand_t[:], in_=cand)
-        load_scale_rows(nc.sync, v_table_plane, v_scales[0])
         load_words(nc, v_table, v_words)
 
         nc.scalar.activation(out=warm[:, 1:2], in_=warm[:, 0:1], func=SIGMOID)
@@ -145,6 +148,8 @@ def tile_picked_zcbow_sig_p_kernel(
                 nc.scalar.copy(out=h[m][:, cols], in_=h_ps[:])
 
         project(0, (0, 1), w0)
+        v_rows = sbuf("v_rows", [P, R], U8)
+        nc.vector.tensor_copy(out=v_rows[:], in_=v_table_plane[:].indirect(cand_t[:]))
         codes1 = quantise("w1", grouped1)
 
         terms = {}
@@ -209,6 +214,8 @@ def tile_picked_zcbow_sig_p_kernel(
         term(sums1, 0)
         h[3] = sbuf("h3", [P, S], F32)
         project(3, (5, 6), quantise("w3", cast_w(3, "w_grouped2")))
+        v_plane = sbuf("v_plane", [P, R], U8, "w2_codes")
+        load_scale_rows(nc.sync, v_plane, v_rows)
         pair = sbuf("term1_pair", [P, 2 * V], F32, "w_raw3")
         term(sums1, 1, part=pair[:, 0:V])
         term(sums1, 2, part=pair[:, V : 2 * V])
@@ -224,19 +231,16 @@ def tile_picked_zcbow_sig_p_kernel(
         def score(b, a, number, queue, after=None):
             cols = HALVES[a]
             y_ps = bank(number, [P, HALF], f"y_ps{b}_{a}")
-            product(y_ps[:], *z[b], v_codes[a][:], v_plane[:, cols])
+            product(y_ps[:], *z[b], v_codes[:, cols], v_plane[:, cols])
             result = sbuf(f"result{b}_{a}", [P, HALF], F32, after)
             nc.scalar.activation(out=result[:], in_=y_ps[:], func=SIGMOID)
             queue.dma_start(out=out[b * P : (b + 1) * P, cols], in_=result[:])
 
-        v_codes = [sbuf("v_codes0", [P, HALF], U32, "term3_1_0"), sbuf("v_codes1", [P, HALF], U32, "z_grouped0")]
-        nc.vector.tensor_copy(out=v_codes[0][:], in_=v_table[:].indirect(entries(cand_t, HALVES[0])))
-        v_plane = sbuf("v_plane", [P, R], U8, "term3_0_2")
-        nc.vector.tensor_copy(out=v_plane[:], in_=v_table_plane[:].indirect(cand_t[:]))
-        z = [quantise("z0", z_grouped0)]
+        v_codes = sbuf("v_codes", [P, R], U32, "term3_1_0")
+        nc.vector.tensor_copy(out=v_codes[:], in_=v_table[:].indirect(cand_t[:]))
+        z = [quantise("z0", z_grouped0, 8192)]
         score(0, 0, 1, nc.sync, "w3_codes")
-        nc.vector.tensor_copy(out=v_codes[1][:], in_=v_table[:].indirect(entries(cand_t, HALVES[1])))
-        z.append(quantise("z1", z_grouped1))
         score(0, 1, 2, nc.sync)
+        z.append(quantise("z1", z_grouped1, 8704))
         score(1, 0, 3, nc.sync)
         score(1, 1, 4, nc.sync)

@@ -22,6 +22,7 @@ QUADRANT = 32
 LIST_ROWS = 16
 ROW_TILES = H // P
 SCALE_ROWS = 16
+BLOCK_ROWS = 8
 HALF = 256
 HALVES = (slice(0, HALF), slice(HALF, 2 * HALF))
 
@@ -99,12 +100,12 @@ def tile_picked_zcbow_sig_p_kernel(
         nc.gpsimd.memset(x_table_plane[:].bitcast(I32), 0)
         nc.gpsimd.memset(warm[:], 0.0)
         nc.gpsimd.memset(v_table_plane[:].bitcast(I32), 0)
-        nc.gpsimd.dma_start(out=v_table_plane[0:SCALE_ROWS, :].bitcast(I32), in_=v_scales[0].bitcast(I32))
+        nc.gpsimd.dma_start(out=v_table_plane[0:P:BLOCK_ROWS, :].bitcast(I32), in_=v_scales[0].bitcast(I32))
         make_identity(nc, ident[:])
 
         w_rows = w1.rearrange("(p j) c -> p j c", j=PACK)
-        nc.sync.dma_start(out=offs_t[:], in_=offs)
         load_words(nc, x_table, x_words)
+        nc.sync.dma_start(out=offs_t[:], in_=offs)
         load_scale_rows(nc.sync, x_table_plane, x_scales[0])
         nc.sync.dma_start(out=w_raw[0], in_=w_rows[:, :, 0:P])
         nc.sync.dma_start(out=w_raw[1], in_=w_rows[:, :, P : 2 * P])
@@ -215,7 +216,7 @@ def tile_picked_zcbow_sig_p_kernel(
         h[3] = sbuf("h3", [P, S], F32)
         project(3, (5, 6), quantise("w3", cast_w(3, "w_grouped2")))
         v_plane = sbuf("v_plane", [P, R], U8, "w2_codes")
-        load_scale_rows(nc.sync, v_plane, v_rows)
+        load_scale_rows(nc.sync, v_plane, v_rows[0:P:BLOCK_ROWS, :])
         pair = sbuf("term1_pair", [P, 2 * V], F32, "w_raw3")
         term(sums1, 1, part=pair[:, 0:V])
         term(sums1, 2, part=pair[:, V : 2 * V])
@@ -223,24 +224,45 @@ def tile_picked_zcbow_sig_p_kernel(
         round_z(*sums0)
         round_z(*sums1)
         round_z(*windows(2, [0, 1], 4))
-        round_z(*windows(3, [0], 5))
-        round_z(*windows(3, [1], 6))
+        last = [sums(3, [b], 5 + b) for b in range(2)]
+        both = sbuf("term3_0", [P, V], F32)
+        nc.vector.tensor_tensor(out=both[:], in0=h[3][:].indirect(pos_t[0][:]), in1=gate_t[:, 0, :], op=MULT)
+        for b in range(2):
+            nc.tensor.matmul(
+                out=last[b][2][:, 0, :],
+                lhsT=both[:, b * P : (b + 1) * P],
+                rhs=ident[:],
+                is_transpose=True,
+                start=True,
+                stop=False,
+            )
+        for b in range(2):
+            for d in range(1, D):
+                term(last[b], d)
+            round_z(*last[b])
         z_grouped0 = turn_z(0, 7)
         z_grouped1 = turn_z(1, 0)
 
-        def score(b, a, number, queue, after=None):
-            cols = HALVES[a]
-            y_ps = bank(number, [P, HALF], f"y_ps{b}_{a}")
+        def score(b, cols, number, result):
+            y_ps = bank(number, [P, cols.stop - cols.start], f"y_ps{b}_{cols.start}")
             product(y_ps[:], *z[b], v_codes[:, cols], v_plane[:, cols])
-            result = sbuf(f"result{b}_{a}", [P, HALF], F32, after)
-            nc.scalar.activation(out=result[:], in_=y_ps[:], func=SIGMOID)
-            queue.dma_start(out=out[b * P : (b + 1) * P, cols], in_=result[:])
+            nc.scalar.activation(out=result, in_=y_ps[:], func=SIGMOID)
 
-        v_codes = sbuf("v_codes", [P, R], U32, "term3_1_0")
+        def store(b, cols, result):
+            nc.sync.dma_start(out=out[b * P : (b + 1) * P, cols], in_=result)
+
+        v_codes = sbuf("v_codes", [P, R], U32, "term3_0_2")
         nc.vector.tensor_copy(out=v_codes[:], in_=v_table[:].indirect(cand_t[:]))
-        z = [quantise("z0", z_grouped0, 8192)]
-        score(0, 0, 1, nc.sync, "w3_codes")
-        score(0, 1, 2, nc.sync)
-        z.append(quantise("z1", z_grouped1, 8704))
-        score(1, 0, 3, nc.sync)
-        score(1, 1, 4, nc.sync)
+        z = [quantise("z0", z_grouped0)]
+        result0 = sbuf("result0", [P, R], F32, "w3_codes")
+        for a, cols in enumerate(HALVES):
+            score(0, cols, 1 + a, result0[:, cols])
+            store(0, cols, result0[:, cols])
+        z.append(quantise("z1", z_grouped1))
+        result1 = sbuf("result1", [P, R], F32)
+        for a in range(R // P):
+            cols = slice(a * P, (a + 1) * P)
+            score(1, cols, 3 + a, result1[:, cols])
+            if a % 2 == 1:
+                ready = HALVES[a // 2]
+                store(1, ready, result1[:, ready])

@@ -19,21 +19,24 @@ SIGMOID = mybir.ActivationFunctionType.Sigmoid
 P = 128
 PACK = 4
 QUADRANT = 32
-LIST_ROWS = 16
-ROW_TILES = H // P
 SCALE_ROWS = 16
-BLOCK_ROWS = 8
+ROW_STEP = P // SCALE_ROWS
+LIST_ROWS = 16
 HALF = 256
 HALVES = (slice(0, HALF), slice(HALF, 2 * HALF))
+EARLY, LATE = slice(0, S - P), slice(S - P, S)
+KIB = 1024
+RAW2_AT, TERM02_AT, H1_AT = 0, 0, KIB
+RAW3_AT, TERMS1_AT, H2_AT = 4 * KIB, 3 * KIB, 5 * KIB
 
 
-def load_words(nc, tile, words):
-    nc.sync.dma_start(out=tile[:].bitcast(I32), in_=words[0].rearrange("p n t -> p (n t)").bitcast(I32))
+def as_words(words):
+    return words[0].rearrange("p n t -> p (n t)").bitcast(I32)
 
 
-def load_scale_rows(queue, plane, scales):
+def spread_scale_rows(nc, plane, rows):
     for r in range(PACK):
-        queue.dma_start(out=plane[r:P:QUADRANT, :].bitcast(I32), in_=scales[r:SCALE_ROWS:PACK, :].bitcast(I32))
+        nc.sync.dma_start(out=plane[r:P:QUADRANT, :].bitcast(I32), in_=rows[r:SCALE_ROWS:PACK, :].bitcast(I32))
 
 
 def entries(offsets, cols):
@@ -52,8 +55,8 @@ def tile_picked_zcbow_sig_p_kernel(
         def sbuf(name, shape, dtype, after=None):
             return keep.tile(shape, dtype, name=name, tag=after or name, align_bytes=64)
 
-        def placed(name, shape, offset, dtype=F32):
-            return shared.tile(shape, dtype, name=name, offset=offset, align_bytes=64)
+        def placed(name, shape, offset):
+            return shared.tile(shape, F32, name=name, offset=offset, align_bytes=64)
 
         def bank(number, shape, name):
             return psum.tile(shape, F32, name=name, tag=f"bank{number}")
@@ -69,18 +72,12 @@ def tile_picked_zcbow_sig_p_kernel(
                 stop=True,
             )
 
-        made = {}
-
-        def quantise(name, grouped, offset=None):
-            if offset is None:
-                codes = sbuf(f"{name}_codes", [P, P], U32)
-            else:
-                codes = placed(f"{name}_codes", [P, P], offset, U32)
+        def quantise(name, grouped):
+            codes = sbuf(f"{name}_codes", [P, P], U32)
             plane = sbuf(f"{name}_plane", [P, P], U8)
             nc.vector.quantize_mx(
                 out=codes[:].bitcast(FP8X4), scales=plane[:], in_=grouped[:].rearrange("p c j -> p (c j)")
             )
-            made[name] = codes
             return codes[:], plane[:]
 
         offs_t = sbuf("offs_t", [P, S // LIST_ROWS], U16)
@@ -88,109 +85,95 @@ def tile_picked_zcbow_sig_p_kernel(
         pos_t = [sbuf(f"pos_t{d}", [P, V // LIST_ROWS], U16) for d in range(D)]
         x_table = sbuf("x_table", [P, T], U32)
         x_table_plane = sbuf("x_table_plane", [P, T], U8)
-        v_table = placed("v_table", [P, G], 8192, U32)
-        v_table_plane = sbuf("v_table_plane", [P, G], U8)
+        v_table = sbuf("v_table", [P, G], U32)
+        v_table_rows = sbuf("v_table_rows", [P, G], U8)
         gate_t = sbuf("gate_t", [P, D, V], F32)
-        w_raw = [sbuf(f"w_raw{m}", [P, PACK, P], F32)[:] for m in range(2)]
-        w_raw.append(placed("w_raw2", [P, PACK, P], 0)[:])
-        w_raw.append(sbuf("w_raw3", [P, PACK, P], F32)[:])
+        w_raw = [sbuf(f"w_raw{m}", [P, PACK, P], F32) for m in range(2)]
+        w_raw.extend([placed("w_raw2", [P, PACK, P], RAW2_AT), placed("w_raw3", [P, PACK, P], RAW3_AT)])
         ident = sbuf("ident", [P, P], F32)
         warm = sbuf("warm", [P, 8], F32)
 
         nc.gpsimd.memset(x_table_plane[:].bitcast(I32), 0)
         nc.gpsimd.memset(warm[:], 0.0)
-        nc.gpsimd.memset(v_table_plane[:].bitcast(I32), 0)
-        nc.gpsimd.dma_start(out=v_table_plane[0:P:BLOCK_ROWS, :].bitcast(I32), in_=v_scales[0].bitcast(I32))
+        nc.gpsimd.memset(v_table_rows[:].bitcast(I32), 0)
+        nc.gpsimd.dma_start(out=v_table_rows[0:P:ROW_STEP, :].bitcast(I32), in_=v_scales[0].bitcast(I32))
         make_identity(nc, ident[:])
 
         w_rows = w1.rearrange("(p j) c -> p j c", j=PACK)
-        load_words(nc, x_table, x_words)
+
+        def load_w(m):
+            nc.sync.dma_start(out=w_raw[m][:], in_=w_rows[:, :, m * P : (m + 1) * P])
+
+        nc.sync.dma_start(out=x_table[:].bitcast(I32), in_=as_words(x_words))
         nc.sync.dma_start(out=offs_t[:], in_=offs)
-        load_scale_rows(nc.sync, x_table_plane, x_scales[0])
-        nc.sync.dma_start(out=w_raw[0], in_=w_rows[:, :, 0:P])
-        nc.sync.dma_start(out=w_raw[1], in_=w_rows[:, :, P : 2 * P])
+        spread_scale_rows(nc, x_table_plane, x_scales[0])
+        load_w(0)
+        load_w(1)
         nc.sync.dma_start(out=cand_t[:], in_=cand)
         nc.sync.dma_start(out=gate_t[:], in_=gate.rearrange("d p t -> p d t"))
-        for d, pos in enumerate((pos1, pos2, pos3)):
-            nc.sync.dma_start(out=pos_t[d][:], in_=pos)
-        for m in range(2, ROW_TILES):
-            nc.sync.dma_start(out=w_raw[m], in_=w_rows[:, :, m * P : (m + 1) * P])
-        load_words(nc, v_table, v_words)
+        nc.sync.dma_start(out=pos_t[0][:], in_=pos1)
+        load_w(2)
+        nc.sync.dma_start(out=pos_t[1][:], in_=pos2)
+        nc.sync.dma_start(out=pos_t[2][:], in_=pos3)
+        load_w(3)
+        nc.sync.dma_start(out=v_table[:].bitcast(I32), in_=as_words(v_words))
 
         nc.scalar.activation(out=warm[:, 1:2], in_=warm[:, 0:1], func=SIGMOID)
 
-        def cast_w(m, after=None):
-            grouped = sbuf(f"w_grouped{m}", [P, P, PACK], BF16, after)
+        def cast_w(m):
+            grouped = sbuf(f"w_grouped{m}", [P, P, PACK], BF16)
             nc.scalar.copy(
                 out=grouped[:].rearrange("p (c i) j -> p c j i", i=PACK),
-                in_=w_raw[m].rearrange("p j (c i) -> p c j i", i=PACK),
+                in_=w_raw[m][:].rearrange("p j (c i) -> p c j i", i=PACK),
             )
             return grouped
 
-        h = {0: sbuf("h0", [P, S], F32)}
         x_codes = sbuf("x_codes", [P, S], U32)
         nc.vector.tensor_copy(out=x_codes[:], in_=x_table[:].indirect(offs_t[:]))
-        early, late = slice(0, S - P), slice(S - P, S)
         x_plane = sbuf("x_plane", [P, S - P], U8)
         x_plane_late = sbuf("x_plane_late", [P, P], U8, "w_raw0")
-        nc.vector.tensor_copy(out=x_plane[:], in_=x_table_plane[:].indirect(entries(offs_t, early)))
-        w0 = quantise("w0", cast_w(0))
-        nc.vector.tensor_copy(out=x_plane_late[:], in_=x_table_plane[:].indirect(entries(offs_t, late)))
+        nc.vector.tensor_copy(out=x_plane[:], in_=x_table_plane[:].indirect(entries(offs_t, EARLY)))
+        w_mx = {0: quantise("w0", cast_w(0))}
+        nc.vector.tensor_copy(out=x_plane_late[:], in_=x_table_plane[:].indirect(entries(offs_t, LATE)))
         grouped1 = cast_w(1)
 
-        def project(m, banks, grouped_or_codes):
-            for a, cols in enumerate(HALVES):
-                h_ps = bank(banks[a], [P, HALF], f"h_ps{m}_{a}")
-                if a == 0:
-                    product(h_ps[:], *grouped_or_codes, x_codes[:, cols], x_plane[:, cols])
-                else:
-                    product(h_ps[:, 0:P], *grouped_or_codes, x_codes[:, HALF : S - P], x_plane[:, HALF : S - P])
-                    product(h_ps[:, P:HALF], *grouped_or_codes, x_codes[:, late], x_plane_late[:])
-                nc.scalar.copy(out=h[m][:, cols], in_=h_ps[:])
+        h = {}
 
-        project(0, (0, 1), w0)
+        def project(m, tile, banks):
+            h[m] = tile
+            low = bank(banks[0], [P, HALF], f"h_low{m}")
+            product(low[:], *w_mx[m], x_codes[:, HALVES[0]], x_plane[:, HALVES[0]])
+            nc.scalar.copy(out=tile[:, HALVES[0]], in_=low[:])
+            high = bank(banks[1], [P, HALF], f"h_high{m}")
+            product(high[:, 0:P], *w_mx[m], x_codes[:, HALF : EARLY.stop], x_plane[:, HALF : EARLY.stop])
+            product(high[:, P:HALF], *w_mx[m], x_codes[:, LATE], x_plane_late[:])
+            nc.scalar.copy(out=tile[:, HALVES[1]], in_=high[:])
+
+        project(0, sbuf("h0", [P, S], F32), (0, 1))
         v_rows = sbuf("v_rows", [P, R], U8)
-        nc.vector.tensor_copy(out=v_rows[:], in_=v_table_plane[:].indirect(cand_t[:]))
-        codes1 = quantise("w1", grouped1)
+        nc.vector.tensor_copy(out=v_rows[:], in_=v_table_rows[:].indirect(cand_t[:]))
+        w_mx[1] = quantise("w1", grouped1)
 
-        terms = {}
-
-        def sums(m, blocks, number):
-            return m, blocks, bank(number, [P, len(blocks), P], f"zt_ps{m}_{blocks[0]}")
-
-        def term(group, d, after=None, part=None):
-            m, blocks, zt_ps = group
-            n = len(blocks)
-            cols = slice(blocks[0] * P, (blocks[-1] + 1) * P)
-            if part is None:
-                part = sbuf(f"term{m}_{blocks[0]}_{d}", [P, n * P], F32, after)
-            terms[m, blocks[0], d] = part
+        def gather_term(m, d, cols, part):
             nc.vector.tensor_tensor(
-                out=part[:], in0=h[m][:].indirect(entries(pos_t[d], cols)), in1=gate_t[:, d, cols], op=MULT
+                out=part, in0=h[m][:].indirect(entries(pos_t[d], cols)), in1=gate_t[:, d, cols], op=MULT
             )
-            for a in range(n):
-                nc.tensor.matmul(
-                    out=zt_ps[:, a, :],
-                    lhsT=part[:, a * P : (a + 1) * P],
-                    rhs=ident[:],
-                    is_transpose=True,
-                    start=(d == 0 and a == 0),
-                    stop=(d == D - 1 and a == n - 1),
-                )
 
-        def windows(m, blocks, number):
-            group = sums(m, blocks, number)
-            for d in range(D):
-                term(group, d)
-            return group
+        def add_turned(sums, part, start, stop):
+            nc.tensor.matmul(out=sums, lhsT=part, rhs=ident[:], is_transpose=True, start=start, stop=stop)
 
-        def round_z(m, blocks, zt_ps):
-            words_here = slice(m * P // PACK, (m + 1) * P // PACK)
-            for a in range(len(blocks)):
-                nc.scalar.copy(
-                    out=zt[blocks[a]][:, :, words_here, :],
-                    in_=zt_ps[:, a, :].rearrange("t (p u e) -> t u p e", u=2, e=2),
-                )
+        def both_blocks(m, d, sums, part=None):
+            if part is None:
+                part = sbuf(f"term{m}_{d}", [P, V], F32)[:]
+            gather_term(m, d, slice(0, V), part)
+            for b in range(2):
+                add_turned(sums[:, b, :], part[:, b * P : (b + 1) * P], d == 0 and b == 0, d == D - 1 and b == 1)
+
+        def round_z(m, b, sums):
+            nc.scalar.copy(
+                out=zt[b][:, :, m * P // PACK : (m + 1) * P // PACK, :],
+                in_=sums.rearrange("t (p u e) -> t u p e", u=2, e=2),
+            )
 
         def turn_z(b, number):
             pairs = zt[b][:].rearrange("t u p e -> t (u p e)").bitcast(F32)
@@ -202,67 +185,66 @@ def tile_picked_zcbow_sig_p_kernel(
             nc.scalar.copy(out=grouped_pairs, in_=z_ps[:].rearrange("p u t -> p t u"))
             return grouped
 
-        sums0 = sums(0, [0, 1], 3)
-        term(sums0, 0)
-        term(sums0, 1)
+        sums = {0: bank(3, [P, 2, P], "sums0")}
+        both_blocks(0, 0, sums[0])
+        both_blocks(0, 1, sums[0])
         grouped2 = cast_w(2)
-        h[1] = placed("h1", [P, S], 1024)
-        project(1, (2, 4), codes1)
-        h[2] = sbuf("h2", [P, S], F32)
-        project(2, (0, 1), quantise("w2", grouped2))
-        term(sums0, 2, part=placed("term0_2", [P, V], 0)[:])
-        sums1 = sums(1, [0, 1], 2)
-        term(sums1, 0)
-        h[3] = sbuf("h3", [P, S], F32)
-        project(3, (5, 6), quantise("w3", cast_w(3, "w_grouped2")))
+        project(1, placed("h1", [P, S], H1_AT), (2, 4))
+        w_mx[2] = quantise("w2", grouped2)
+        both_blocks(0, 2, sums[0], placed("term0_2", [P, V], TERM02_AT)[:])
+        sums[1] = bank(2, [P, 2, P], "sums1")
+        both_blocks(1, 0, sums[1])
+        grouped3 = cast_w(3)
+        project(2, placed("h2", [P, S], H2_AT), (0, 1))
+        w_mx[3] = quantise("w3", grouped3)
+        project(3, sbuf("h3", [P, S], F32), (5, 6))
         v_plane = sbuf("v_plane", [P, R], U8, "w2_codes")
-        load_scale_rows(nc.sync, v_plane, v_rows[0:P:BLOCK_ROWS, :])
-        pair = sbuf("term1_pair", [P, 2 * V], F32, "w_raw3")
-        term(sums1, 1, part=pair[:, 0:V])
-        term(sums1, 2, part=pair[:, V : 2 * V])
-        zt = [sbuf(f"zt{b}", [P, 2, P, 2], BF16, ("w_grouped2", "w3_codes")[b]) for b in range(V // P)]
-        round_z(*sums0)
-        round_z(*sums1)
-        round_z(*windows(2, [0, 1], 4))
-        last = [sums(3, [b], 5 + b) for b in range(2)]
-        both = sbuf("term3_0", [P, V], F32)
-        nc.vector.tensor_tensor(out=both[:], in0=h[3][:].indirect(pos_t[0][:]), in1=gate_t[:, 0, :], op=MULT)
+        spread_scale_rows(nc, v_plane, v_rows[0:P:ROW_STEP, :])
+        terms1 = placed("terms1", [P, D - 1, V], TERMS1_AT)
+        for d in range(1, D):
+            both_blocks(1, d, sums[1], terms1[:, d - 1, :])
+
+        zt = [sbuf("zt0", [P, 2, P, 2], BF16, "w_grouped3"), sbuf("zt1", [P, 2, P, 2], BF16, "w3_codes")]
+        for m in range(2):
+            for b in range(2):
+                round_z(m, b, sums[m][:, b, :])
+        sums[2] = bank(4, [P, 2, P], "sums2")
+        for d in range(D):
+            both_blocks(2, d, sums[2])
         for b in range(2):
-            nc.tensor.matmul(
-                out=last[b][2][:, 0, :],
-                lhsT=both[:, b * P : (b + 1) * P],
-                rhs=ident[:],
-                is_transpose=True,
-                start=True,
-                stop=False,
-            )
+            round_z(2, b, sums[2][:, b, :])
+
+        last = [bank(5 + b, [P, P], f"sums3_{b}") for b in range(2)]
+        first_term = sbuf("term3_0", [P, V], F32)
+        gather_term(3, 0, slice(0, V), first_term[:])
+        for b in range(2):
+            add_turned(last[b][:], first_term[:, b * P : (b + 1) * P], True, False)
         for b in range(2):
             for d in range(1, D):
-                term(last[b], d)
-            round_z(*last[b])
-        z_grouped0 = turn_z(0, 7)
-        z_grouped1 = turn_z(1, 0)
+                part = sbuf(f"term3_{d}_block{b}", [P, P], F32)
+                gather_term(3, d, slice(b * P, (b + 1) * P), part[:])
+                add_turned(last[b][:], part[:], False, d == D - 1)
+            round_z(3, b, last[b][:])
+        z_grouped = [turn_z(0, 7), turn_z(1, 0)]
 
-        def score(b, cols, number, result):
-            y_ps = bank(number, [P, cols.stop - cols.start], f"y_ps{b}_{cols.start}")
-            product(y_ps[:], *z[b], v_codes[:, cols], v_plane[:, cols])
-            nc.scalar.activation(out=result, in_=y_ps[:], func=SIGMOID)
+        def score(z_mx, cols, number, result):
+            y_ps = bank(number, [P, cols.stop - cols.start], f"y_ps{number}")
+            product(y_ps[:], *z_mx, v_codes[:, cols], v_plane[:, cols])
+            nc.scalar.activation(out=result[:, cols], in_=y_ps[:], func=SIGMOID)
 
         def store(b, cols, result):
-            nc.sync.dma_start(out=out[b * P : (b + 1) * P, cols], in_=result)
+            nc.sync.dma_start(out=out[b * P : (b + 1) * P, cols], in_=result[:, cols])
 
-        v_codes = sbuf("v_codes", [P, R], U32, "term3_0_2")
+        v_codes = sbuf("v_codes", [P, R], U32, "term3_2_block0")
         nc.vector.tensor_copy(out=v_codes[:], in_=v_table[:].indirect(cand_t[:]))
-        z = [quantise("z0", z_grouped0)]
+        z0 = quantise("z0", z_grouped[0])
         result0 = sbuf("result0", [P, R], F32, "w3_codes")
         for a, cols in enumerate(HALVES):
-            score(0, cols, 1 + a, result0[:, cols])
-            store(0, cols, result0[:, cols])
-        z.append(quantise("z1", z_grouped1))
+            score(z0, cols, 1 + a, result0)
+            store(0, cols, result0)
+        z1 = quantise("z1", z_grouped[1])
         result1 = sbuf("result1", [P, R], F32)
-        for a in range(R // P):
-            cols = slice(a * P, (a + 1) * P)
-            score(1, cols, 3 + a, result1[:, cols])
-            if a % 2 == 1:
-                ready = HALVES[a // 2]
-                store(1, ready, result1[:, ready])
+        for a, cols in enumerate(HALVES):
+            score(z1, slice(cols.start, cols.start + P), 3 + 2 * a, result1)
+            score(z1, slice(cols.start + P, cols.stop), 4 + 2 * a, result1)
+            store(1, cols, result1)

@@ -72,12 +72,15 @@ def tile_picked_zcbow_sig_p_kernel(
                 stop=True,
             )
 
-        def quantise(name, grouped):
+        def quantise(name, grouped, pieces=(slice(0, P),)):
             codes = sbuf(f"{name}_codes", [P, P], U32)
             plane = sbuf(f"{name}_plane", [P, P], U8)
-            nc.vector.quantize_mx(
-                out=codes[:].bitcast(FP8X4), scales=plane[:], in_=grouped[:].rearrange("p c j -> p (c j)")
-            )
+            for part in pieces:
+                nc.vector.quantize_mx(
+                    out=codes[:, part].bitcast(FP8X4),
+                    scales=plane[:, part],
+                    in_=grouped[:, part, :].rearrange("p c j -> p (c j)"),
+                )
             return codes[:], plane[:]
 
         offs_t = sbuf("offs_t", [P, S // LIST_ROWS], U16)
@@ -175,14 +178,15 @@ def tile_picked_zcbow_sig_p_kernel(
                 in_=sums.rearrange("t (p u e) -> t u p e", u=2, e=2),
             )
 
-        def turn_z(b, number):
+        def turn_z(b, number, pieces):
             pairs = zt[b][:].rearrange("t u p e -> t (u p e)").bitcast(F32)
             z_ps = bank(number, [P, 2, P], f"z_ps{b}")
             for u in range(2):
                 nc.tensor.transpose(z_ps[:, u, :], pairs[:, u * P : (u + 1) * P], ident[:])
             grouped = sbuf(f"z_grouped{b}", [P, P, PACK], BF16)
             grouped_pairs = grouped[:].rearrange("p t j -> p (t j)").bitcast(F32).rearrange("p (t u) -> p t u", u=2)
-            nc.scalar.copy(out=grouped_pairs, in_=z_ps[:].rearrange("p u t -> p t u"))
+            for part in pieces:
+                nc.scalar.copy(out=grouped_pairs[:, part], in_=z_ps[:].rearrange("p u t -> p t u")[:, part])
             return grouped
 
         sums = {0: bank(3, [P, 2, P], "sums0")}
@@ -214,18 +218,15 @@ def tile_picked_zcbow_sig_p_kernel(
         for b in range(2):
             round_z(2, b, sums[2][:, b, :])
 
-        last = [bank(5 + b, [P, P], f"sums3_{b}") for b in range(2)]
-        first_term = sbuf("term3_0", [P, V], F32)
-        gather_term(3, 0, slice(0, V), first_term[:])
         for b in range(2):
-            add_turned(last[b][:], first_term[:, b * P : (b + 1) * P], True, False)
-        for b in range(2):
-            for d in range(1, D):
+            last = bank(5 + b, [P, P], f"sums3_{b}")
+            for d in range(D):
                 part = sbuf(f"term3_{d}_block{b}", [P, P], F32)
                 gather_term(3, d, slice(b * P, (b + 1) * P), part[:])
-                add_turned(last[b][:], part[:], False, d == D - 1)
-            round_z(3, b, last[b][:])
-        z_grouped = [turn_z(0, 7), turn_z(1, 0)]
+                add_turned(last[:], part[:], d == 0, d == D - 1)
+            round_z(3, b, last[:])
+        window_halves = (slice(0, P // 2), slice(P // 2, P))
+        z_grouped = [turn_z(0, 7, [slice(0, P)]), turn_z(1, 0, window_halves)]
 
         def score(z_mx, cols, number, result):
             y_ps = bank(number, [P, cols.stop - cols.start], f"y_ps{number}")
@@ -235,14 +236,16 @@ def tile_picked_zcbow_sig_p_kernel(
         def store(b, cols, result):
             nc.sync.dma_start(out=out[b * P : (b + 1) * P, cols], in_=result[:, cols])
 
-        v_codes = sbuf("v_codes", [P, R], U32, "term3_2_block0")
+        v_codes = sbuf("v_codes", [P, R], U32, "term3_0_block1")
         nc.vector.tensor_copy(out=v_codes[:], in_=v_table[:].indirect(cand_t[:]))
         z0 = quantise("z0", z_grouped[0])
         result0 = sbuf("result0", [P, R], F32, "w3_codes")
-        for a, cols in enumerate(HALVES):
-            score(z0, cols, 1 + a, result0)
-            store(0, cols, result0)
-        z1 = quantise("z1", z_grouped[1])
+        score(z0, slice(0, P), 1, result0)
+        score(z0, slice(P, HALF), 2, result0)
+        store(0, HALVES[0], result0)
+        score(z0, HALVES[1], 7, result0)
+        store(0, HALVES[1], result0)
+        z1 = quantise("z1", z_grouped[1], window_halves)
         result1 = sbuf("result1", [P, R], F32)
         for a, cols in enumerate(HALVES):
             score(z1, slice(cols.start, cols.start + P), 3 + 2 * a, result1)

@@ -15,6 +15,7 @@ U8 = mybir.dt.uint8
 FP8X4 = mybir.dt.float8_e4m3fn_x4
 MULT = mybir.AluOpType.mult
 SIGMOID = mybir.ActivationFunctionType.Sigmoid
+COPY = mybir.ActivationFunctionType.Copy
 
 P = 128
 PACK = 4
@@ -24,10 +25,20 @@ ROW_STEP = P // SCALE_ROWS
 LIST_ROWS = 16
 HALF = 256
 HALVES = (slice(0, HALF), slice(HALF, 2 * HALF))
+BLOCKS = (slice(0, P), slice(P, V))
+ALL = slice(0, V)
 EARLY, LATE = slice(0, S - P), slice(S - P, S)
 KIB = 1024
-RAW2_AT, TERM02_AT, H1_AT = 0, 0, KIB
-RAW3_AT, TERMS1_AT, H2_AT = 4 * KIB, 3 * KIB, 5 * KIB
+EDGE = 64
+RAW3_AT = 6 * KIB
+H2_AT = RAW3_AT - 2 * KIB + EDGE
+TERM11_AT = RAW3_AT + EDGE
+FETCHED_AT = TERM11_AT + KIB
+PLANE2_AT = RAW3_AT + 2 * KIB + EDGE
+TERM30_AT = 14 * KIB
+TERM30_LATE_AT = TERM30_AT - KIB // 2 + EDGE
+TERM31_LATE_AT = TERM30_AT + EDGE
+V_CODES_AT = TERM30_LATE_AT - 2 * KIB + EDGE
 
 
 def as_words(words):
@@ -55,8 +66,8 @@ def tile_picked_zcbow_sig_p_kernel(
         def sbuf(name, shape, dtype, after=None):
             return keep.tile(shape, dtype, name=name, tag=after or name, align_bytes=64)
 
-        def placed(name, shape, offset):
-            return shared.tile(shape, F32, name=name, offset=offset, align_bytes=64)
+        def placed(name, shape, offset, dtype=F32):
+            return shared.tile(shape, dtype, name=name, offset=offset, align_bytes=64)
 
         def bank(number, shape, name):
             return psum.tile(shape, F32, name=name, tag=f"bank{number}")
@@ -72,9 +83,12 @@ def tile_picked_zcbow_sig_p_kernel(
                 stop=True,
             )
 
-        def quantise(name, grouped, pieces=(slice(0, P),)):
+        def quantise(name, grouped, pieces=(slice(0, P),), plane_at=None):
             codes = sbuf(f"{name}_codes", [P, P], U32)
-            plane = sbuf(f"{name}_plane", [P, P], U8)
+            if plane_at is None:
+                plane = sbuf(f"{name}_plane", [P, P], U8)
+            else:
+                plane = placed(f"{name}_plane", [P, P], plane_at, U8)
             for part in pieces:
                 nc.vector.quantize_mx(
                     out=codes[:, part].bitcast(FP8X4),
@@ -91,8 +105,8 @@ def tile_picked_zcbow_sig_p_kernel(
         v_table = sbuf("v_table", [P, G], U32)
         v_table_rows = sbuf("v_table_rows", [P, G], U8)
         gate_t = sbuf("gate_t", [P, D, V], F32)
-        w_raw = [sbuf(f"w_raw{m}", [P, PACK, P], F32) for m in range(2)]
-        w_raw.extend([placed("w_raw2", [P, PACK, P], RAW2_AT), placed("w_raw3", [P, PACK, P], RAW3_AT)])
+        w_raw = [sbuf(f"w_raw{m}", [P, PACK, P], F32) for m in range(3)]
+        w_raw.append(placed("w_raw3", [P, PACK, P], RAW3_AT))
         ident = sbuf("ident", [P, P], F32)
         warm = sbuf("warm", [P, 8], F32)
 
@@ -141,6 +155,7 @@ def tile_picked_zcbow_sig_p_kernel(
         grouped1 = cast_w(1)
 
         h = {}
+        terms = {}
 
         def project(m, tile, banks):
             h[m] = tile
@@ -152,31 +167,94 @@ def tile_picked_zcbow_sig_p_kernel(
             product(high[:, P:HALF], *w_mx[m], x_codes[:, LATE], x_plane_late[:])
             nc.scalar.copy(out=tile[:, HALVES[1]], in_=high[:])
 
-        project(0, sbuf("h0", [P, S], F32), (0, 1))
-        v_rows = sbuf("v_rows", [P, R], U8)
-        nc.vector.tensor_copy(out=v_rows[:], in_=v_table_rows[:].indirect(cand_t[:]))
-        w_mx[1] = quantise("w1", grouped1)
-
         def gather_term(m, d, cols, part):
             nc.vector.tensor_tensor(
                 out=part, in0=h[m][:].indirect(entries(pos_t[d], cols)), in1=gate_t[:, d, cols], op=MULT
             )
 
+        def fetch(m, part):
+            nc.scalar.activation(out=part, in_=h[m][:].indirect(pos_t[D - 1][:]), func=COPY)
+
         def add_turned(sums, part, start, stop):
             nc.tensor.matmul(out=sums, lhsT=part, rhs=ident[:], is_transpose=True, start=start, stop=stop)
 
-        def both_blocks(m, d, sums, part=None):
+        sums = [bank(2 + b, [P, 3, P], f"sums{b}") for b in range(2)]
+
+        def add_term(m, part, start=False, stop=False):
+            for b in range(2):
+                add_turned(sums[b][:, m, :], part[:, BLOCKS[b]], start, stop)
+
+        def fused(m, d, part=None, start=False):
             if part is None:
                 part = sbuf(f"term{m}_{d}", [P, V], F32)[:]
-            gather_term(m, d, slice(0, V), part)
-            for b in range(2):
-                add_turned(sums[:, b, :], part[:, b * P : (b + 1) * P], d == 0 and b == 0, d == D - 1 and b == 1)
+            gather_term(m, d, ALL, part)
+            terms[m, d] = part
+            add_term(m, part, start=start)
 
-        def round_z(m, b, sums):
-            nc.scalar.copy(
-                out=zt[b][:, :, m * P // PACK : (m + 1) * P // PACK, :],
-                in_=sums.rearrange("t (p u e) -> t u p e", u=2, e=2),
+        def weigh(name, fetched, count):
+            term = sbuf(name, [P, count, V], F32)
+            nc.vector.tensor_tensor(
+                out=term[:], in0=fetched, in1=gate_t[:, D - 1 : D, :].to_broadcast([P, count, V]), op=MULT
             )
+            return term
+
+        project(0, sbuf("h0", [P, S], F32), (0, 1))
+        w_mx[1] = quantise("w1", grouped1)
+        v_rows = sbuf("v_rows", [P, R], U8, "w_raw1")
+        nc.vector.tensor_copy(out=v_rows[:], in_=v_table_rows[:].indirect(cand_t[:]))
+        project(1, sbuf("h1", [P, S], F32), (4, 5))
+
+        fused(0, 0, start=True)
+        fused(1, 0)
+        w_mx[2] = quantise("w2", cast_w(2), plane_at=PLANE2_AT)
+        fused(0, 1, sbuf("term0_1", [P, V], F32, "w_raw2")[:])
+        fetched0 = sbuf("fetched0", [P, 1, V], F32)
+        fetch(0, fetched0[:, 0, :])
+        add_term(0, weigh("term0_2", fetched0[:], 1)[:, 0, :])
+        grouped3 = cast_w(3)
+        project(2, placed("h2", [P, S], H2_AT), (0, 1))
+        w_mx[3] = quantise("w3", grouped3)
+        v_plane = sbuf("v_plane", [P, R], U8, "w2_codes")
+        spread_scale_rows(nc, v_plane, v_rows[0:P:ROW_STEP, :])
+        fused(1, 1, placed("term1_1", [P, V], TERM11_AT)[:])
+        fetched12 = placed("fetched12", [P, 2, V], FETCHED_AT)
+        fetch(1, fetched12[:, 0, :])
+        fetch(2, fetched12[:, 1, :])
+        project(3, sbuf("h3", [P, S], F32), (1, 0))
+        fused(2, 0)
+        fused(2, 1)
+        terms12 = weigh("terms12", fetched12[:], 2)
+        add_term(1, terms12[:, 0, :])
+        add_term(2, terms12[:, 1, :], stop=True)
+        fetched3 = sbuf("fetched3", [P, 1, V], F32)
+        fetch(3, fetched3[:, 0, :])
+
+        zt = [sbuf(f"zt{b}", [P, 2, P, 2], BF16) for b in range(2)]
+
+        def round_z(b, first, sums_in):
+            count = sums_in.shape[1] // PACK
+            nc.scalar.copy(
+                out=zt[b][:, :, first : first + count, :],
+                in_=sums_in.rearrange("t (p u e) -> t u p e", u=2, e=2),
+            )
+
+        for b in range(2):
+            round_z(b, 0, sums[b][:].rearrange("t m i -> t (m i)"))
+
+        last = [bank(6 + b, [P, P], f"last{b}") for b in range(2)]
+        first_parts = [placed("term3_0_block0", [P, P], TERM30_AT), sbuf("term3_1_block0", [P, P], F32)]
+        for d in range(2):
+            gather_term(3, d, BLOCKS[0], first_parts[d][:])
+            add_turned(last[0][:], first_parts[d][:], d == 0, False)
+        term3_2 = weigh("term3_2", fetched3[:], 1)
+        add_turned(last[0][:], term3_2[:, 0, BLOCKS[0]], False, True)
+        add_turned(last[1][:], term3_2[:, 0, BLOCKS[1]], True, False)
+        round_z(0, 3 * P // PACK, last[0][:])
+        second_parts = [placed("term3_0_block1", [P, P], TERM30_LATE_AT), placed("term3_1_block1", [P, P], TERM31_LATE_AT)]
+        for d in range(2):
+            gather_term(3, d, BLOCKS[1], second_parts[d][:])
+            add_turned(last[1][:], second_parts[d][:], False, d == 1)
+        round_z(1, 3 * P // PACK, last[1][:])
 
         def turn_z(b, number, pieces):
             pairs = zt[b][:].rearrange("t u p e -> t (u p e)").bitcast(F32)
@@ -189,44 +267,8 @@ def tile_picked_zcbow_sig_p_kernel(
                 nc.scalar.copy(out=grouped_pairs[:, part], in_=z_ps[:].rearrange("p u t -> p t u")[:, part])
             return grouped
 
-        sums = {0: bank(3, [P, 2, P], "sums0")}
-        both_blocks(0, 0, sums[0])
-        both_blocks(0, 1, sums[0])
-        grouped2 = cast_w(2)
-        project(1, placed("h1", [P, S], H1_AT), (2, 4))
-        w_mx[2] = quantise("w2", grouped2)
-        both_blocks(0, 2, sums[0], placed("term0_2", [P, V], TERM02_AT)[:])
-        sums[1] = bank(2, [P, 2, P], "sums1")
-        both_blocks(1, 0, sums[1])
-        grouped3 = cast_w(3)
-        project(2, placed("h2", [P, S], H2_AT), (0, 1))
-        w_mx[3] = quantise("w3", grouped3)
-        project(3, sbuf("h3", [P, S], F32), (5, 6))
-        v_plane = sbuf("v_plane", [P, R], U8, "w2_codes")
-        spread_scale_rows(nc, v_plane, v_rows[0:P:ROW_STEP, :])
-        terms1 = placed("terms1", [P, D - 1, V], TERMS1_AT)
-        for d in range(1, D):
-            both_blocks(1, d, sums[1], terms1[:, d - 1, :])
-
-        zt = [sbuf("zt0", [P, 2, P, 2], BF16, "w_grouped3"), sbuf("zt1", [P, 2, P, 2], BF16, "w3_codes")]
-        for m in range(2):
-            for b in range(2):
-                round_z(m, b, sums[m][:, b, :])
-        sums[2] = bank(4, [P, 2, P], "sums2")
-        for d in range(D):
-            both_blocks(2, d, sums[2])
-        for b in range(2):
-            round_z(2, b, sums[2][:, b, :])
-
-        for b in range(2):
-            last = bank(5 + b, [P, P], f"sums3_{b}")
-            for d in range(D):
-                part = sbuf(f"term3_{d}_block{b}", [P, P], F32)
-                gather_term(3, d, slice(b * P, (b + 1) * P), part[:])
-                add_turned(last[:], part[:], d == 0, d == D - 1)
-            round_z(3, b, last[:])
         window_halves = (slice(0, P // 2), slice(P // 2, P))
-        z_grouped = [turn_z(0, 7, [slice(0, P)]), turn_z(1, 0, window_halves)]
+        z_grouped = [turn_z(0, 0, [slice(0, P)]), turn_z(1, 1, window_halves)]
 
         def score(z_mx, cols, number, result):
             y_ps = bank(number, [P, cols.stop - cols.start], f"y_ps{number}")
@@ -236,18 +278,18 @@ def tile_picked_zcbow_sig_p_kernel(
         def store(b, cols, result):
             nc.sync.dma_start(out=out[b * P : (b + 1) * P, cols], in_=result[:, cols])
 
-        v_codes = sbuf("v_codes", [P, R], U32, "term3_0_block1")
+        v_codes = placed("v_codes", [P, R], V_CODES_AT, U32)
         nc.vector.tensor_copy(out=v_codes[:], in_=v_table[:].indirect(cand_t[:]))
         z0 = quantise("z0", z_grouped[0])
-        result0 = sbuf("result0", [P, R], F32, "w3_codes")
-        score(z0, slice(0, P), 1, result0)
-        score(z0, slice(P, HALF), 2, result0)
+        result0 = sbuf("result0", [P, R], F32, "zt1")
+        score(z0, slice(0, P), 4, result0)
+        score(z0, slice(P, HALF), 5, result0)
         store(0, HALVES[0], result0)
-        score(z0, HALVES[1], 7, result0)
+        score(z0, HALVES[1], 6, result0)
         store(0, HALVES[1], result0)
         z1 = quantise("z1", z_grouped[1], window_halves)
         result1 = sbuf("result1", [P, R], F32)
         for a, cols in enumerate(HALVES):
-            score(z1, slice(cols.start, cols.start + P), 3 + 2 * a, result1)
-            score(z1, slice(cols.start + P, cols.stop), 4 + 2 * a, result1)
+            score(z1, slice(cols.start, cols.start + P), (2, 7)[a], result1)
+            score(z1, slice(cols.start + P, cols.stop), (3, 0)[a], result1)
             store(1, cols, result1)

@@ -14,6 +14,7 @@ U16 = mybir.dt.uint16
 U8 = mybir.dt.uint8
 FP8X4 = mybir.dt.float8_e4m3fn_x4
 MULT = mybir.AluOpType.mult
+ADD = mybir.AluOpType.add
 SIGMOID = mybir.ActivationFunctionType.Sigmoid
 COPY = mybir.ActivationFunctionType.Copy
 
@@ -127,9 +128,9 @@ def tile_picked_zcbow_sig_p_kernel(
         load_w(0)
         load_w(1)
         nc.sync.dma_start(out=cand_t[:], in_=cand)
+        load_w(2)
         nc.sync.dma_start(out=gate_t[:], in_=gate.rearrange("d p t -> p d t"))
         nc.sync.dma_start(out=pos_t[0][:], in_=pos1)
-        load_w(2)
         nc.sync.dma_start(out=pos_t[1][:], in_=pos2)
         nc.sync.dma_start(out=pos_t[2][:], in_=pos3)
         load_w(3)
@@ -204,10 +205,15 @@ def tile_picked_zcbow_sig_p_kernel(
         nc.vector.tensor_copy(out=v_rows[:], in_=v_table_rows[:].indirect(cand_t[:]))
         project(1, sbuf("h1", [P, S], F32), (4, 5))
 
-        fused(0, 0, start=True)
-        fused(1, 0)
-        w_mx[2] = quantise("w2", cast_w(2), plane_at=PLANE2_AT)
-        fused(0, 1, sbuf("term0_1", [P, V], F32, "w_raw2")[:])
+        grouped2 = sbuf("w_grouped2", [P, P, PACK], BF16)
+        nc.gpsimd.tensor_scalar(
+            out=grouped2[:], in0=w_raw[2][:].rearrange("p j c -> p c j"), scalar1=1.0, scalar2=0.0, op0=MULT, op1=ADD
+        )
+        w_mx[2] = quantise("w2", grouped2, plane_at=PLANE2_AT)
+        first_terms = sbuf("first_terms", [P, 2, V], F32, "w_raw2")
+        fused(0, 0, first_terms[:, 0, :], start=True)
+        fused(1, 0, first_terms[:, 1, :])
+        fused(0, 1)
         fetched0 = sbuf("fetched0", [P, 1, V], F32)
         fetch(0, fetched0[:, 0, :])
         add_term(0, weigh("term0_2", fetched0[:], 1)[:, 0, :])
@@ -217,15 +223,22 @@ def tile_picked_zcbow_sig_p_kernel(
         v_plane = sbuf("v_plane", [P, R], U8, "w2_codes")
         spread_scale_rows(nc, v_plane, v_rows[0:P:ROW_STEP, :])
         fused(1, 1, placed("term1_1", [P, V], TERM11_AT)[:])
-        fetched12 = placed("fetched12", [P, 2, V], FETCHED_AT)
-        fetch(1, fetched12[:, 0, :])
-        fetch(2, fetched12[:, 1, :])
+        fetched12 = placed("fetched12", [P, V + P + V], FETCHED_AT)
+        fetch(1, fetched12[:, 0:V])
+        nc.scalar.activation(out=fetched12[:, V : V + P], in_=h[2][:].indirect(entries(pos_t[1], BLOCKS[1])), func=COPY)
+        fetch(2, fetched12[:, V + P :])
         project(3, sbuf("h3", [P, S], F32), (1, 0))
         fused(2, 0)
-        fused(2, 1)
-        terms12 = weigh("terms12", fetched12[:], 2)
-        add_term(1, terms12[:, 0, :])
-        add_term(2, terms12[:, 1, :], stop=True)
+        term21 = sbuf("term2_1_block0", [P, P], F32)
+        gather_term(2, 1, BLOCKS[0], term21[:])
+        add_turned(sums[0][:, 2, :], term21[:], False, False)
+        add_term(1, weigh("term1_2", fetched12[:, 0:V].rearrange("p (o t) -> p o t", o=1), 1)[:, 0, :])
+        terms12 = sbuf("terms2", [P, P + V], F32)
+        nc.vector.tensor_tensor(
+            out=terms12[:], in0=fetched12[:, V:], in1=gate_t[:].rearrange("p d t -> p (d t)")[:, V + P :], op=MULT
+        )
+        add_turned(sums[1][:, 2, :], terms12[:, 0:P], False, False)
+        add_term(2, terms12[:, P:], stop=True)
         fetched3 = sbuf("fetched3", [P, 1, V], F32)
         fetch(3, fetched3[:, 0, :])
 

@@ -28,18 +28,15 @@ HALF = 256
 HALVES = (slice(0, HALF), slice(HALF, 2 * HALF))
 BLOCKS = (slice(0, P), slice(P, V))
 ALL = slice(0, V)
-EARLY, LATE = slice(0, S - P), slice(S - P, S)
+QUARTERS = tuple(slice(a * P, (a + 1) * P) for a in range(4))
 KIB = 1024
 EDGE = 64
-RAW3_AT = 6 * KIB
-H2_AT = RAW3_AT - 2 * KIB + EDGE
-TERM11_AT = RAW3_AT + EDGE
-FETCHED_AT = TERM11_AT + KIB
-PLANE2_AT = RAW3_AT + 2 * KIB + EDGE
-TERM30_AT = 14 * KIB
-TERM30_LATE_AT = TERM30_AT - KIB // 2 + EDGE
-TERM31_LATE_AT = TERM30_AT + EDGE
-V_CODES_AT = TERM30_LATE_AT - 2 * KIB + EDGE
+PLANE2_AT = 2 * KIB
+FETCHED1_AT = PLANE2_AT - 2 * KIB + EDGE
+PLANE3_AT = 4 * KIB
+FETCHED2_AT = PLANE3_AT - KIB + EDGE
+TERM31_AT = 8 * KIB
+V_CODES_AT = TERM31_AT - 2 * KIB + EDGE
 
 
 def as_words(words):
@@ -84,19 +81,8 @@ def tile_picked_zcbow_sig_p_kernel(
                 stop=True,
             )
 
-        def quantise(name, grouped, pieces=(slice(0, P),), plane_at=None):
-            codes = sbuf(f"{name}_codes", [P, P], U32)
-            if plane_at is None:
-                plane = sbuf(f"{name}_plane", [P, P], U8)
-            else:
-                plane = placed(f"{name}_plane", [P, P], plane_at, U8)
-            for part in pieces:
-                nc.vector.quantize_mx(
-                    out=codes[:, part].bitcast(FP8X4),
-                    scales=plane[:, part],
-                    in_=grouped[:, part, :].rearrange("p c j -> p (c j)"),
-                )
-            return codes[:], plane[:]
+        def quantise(codes, plane, grouped):
+            nc.vector.quantize_mx(out=codes.bitcast(FP8X4), scales=plane, in_=grouped.rearrange("p c j -> p (c j)"))
 
         offs_t = sbuf("offs_t", [P, S // LIST_ROWS], U16)
         cand_t = sbuf("cand_t", [P, R // LIST_ROWS], U16)
@@ -106,8 +92,8 @@ def tile_picked_zcbow_sig_p_kernel(
         v_table = sbuf("v_table", [P, G], U32)
         v_table_rows = sbuf("v_table_rows", [P, G], U8)
         gate_t = sbuf("gate_t", [P, D, V], F32)
-        w_raw = [sbuf(f"w_raw{m}", [P, PACK, P], F32) for m in range(3)]
-        w_raw.append(placed("w_raw3", [P, PACK, P], RAW3_AT))
+        gates = [gate_t[:, d, :] for d in range(D)]
+        w_raw = [sbuf(f"w_raw{m}", [P, PACK, P], F32) for m in range(PACK)]
         ident = sbuf("ident", [P, P], F32)
         warm = sbuf("warm", [P, 8], F32)
 
@@ -127,122 +113,160 @@ def tile_picked_zcbow_sig_p_kernel(
         spread_scale_rows(nc, x_table_plane, x_scales[0])
         load_w(0)
         load_w(1)
-        nc.sync.dma_start(out=cand_t[:], in_=cand)
-        load_w(2)
-        nc.sync.dma_start(out=gate_t[:], in_=gate.rearrange("d p t -> p d t"))
-        nc.sync.dma_start(out=pos_t[0][:], in_=pos1)
         nc.sync.dma_start(out=pos_t[1][:], in_=pos2)
+        load_w(2)
+        nc.sync.dma_start(out=cand_t[:], in_=cand)
         nc.sync.dma_start(out=pos_t[2][:], in_=pos3)
+        nc.sync.dma_start(out=gate_t[:], in_=gate.rearrange("d p t -> p d t"))
         load_w(3)
+        nc.sync.dma_start(out=pos_t[0][:], in_=pos1)
         nc.sync.dma_start(out=v_table[:].bitcast(I32), in_=as_words(v_words))
 
         nc.scalar.activation(out=warm[:, 1:2], in_=warm[:, 0:1], func=SIGMOID)
 
-        def cast_w(m):
-            grouped = sbuf(f"w_grouped{m}", [P, P, PACK], BF16)
-            nc.scalar.copy(
-                out=grouped[:].rearrange("p (c i) j -> p c j i", i=PACK),
-                in_=w_raw[m][:].rearrange("p j (c i) -> p c j i", i=PACK),
+        def by_fours(grouped, m):
+            return (
+                grouped.rearrange("p (c i) j -> p c j i", i=PACK),
+                w_raw[m][:].rearrange("p j (c i) -> p c j i", i=PACK),
             )
-            return grouped
+
+        w_mx = {}
+
+        def grouped_w(m, after=None):
+            return sbuf(f"w_grouped{m}", [P, P, PACK], BF16, after)
+
+        def quantise_w(m, grouped, plane_at=None, after=None):
+            codes = sbuf(f"w_codes{m}", [P, P], U32, after)
+            if plane_at is None:
+                plane = sbuf(f"w_plane{m}", [P, P], U8)
+            else:
+                plane = placed(f"w_plane{m}", [P, P], plane_at, U8)
+            quantise(codes[:], plane[:], grouped[:])
+            w_mx[m] = (codes[:], plane[:])
 
         x_codes = sbuf("x_codes", [P, S], U32)
         nc.vector.tensor_copy(out=x_codes[:], in_=x_table[:].indirect(offs_t[:]))
-        x_plane = sbuf("x_plane", [P, S - P], U8)
-        x_plane_late = sbuf("x_plane_late", [P, P], U8, "w_raw0")
-        nc.vector.tensor_copy(out=x_plane[:], in_=x_table_plane[:].indirect(entries(offs_t, EARLY)))
-        w_mx = {0: quantise("w0", cast_w(0))}
-        nc.vector.tensor_copy(out=x_plane_late[:], in_=x_table_plane[:].indirect(entries(offs_t, LATE)))
-        grouped1 = cast_w(1)
+        x_planes = [sbuf("x_plane0", [P, HALF], U8), sbuf("x_plane1", [P, HALF], U8, "w_raw0")]
+        nc.vector.tensor_copy(out=x_planes[0][:], in_=x_table_plane[:].indirect(entries(offs_t, HALVES[0])))
+        grouped0 = grouped_w(0)
+        nc.scalar.copy(*by_fours(grouped0[:], 0))
+        quantise_w(0, grouped0)
+        for a in range(2):
+            nc.vector.tensor_copy(
+                out=x_planes[1][:, BLOCKS[a]], in_=x_table_plane[:].indirect(entries(offs_t, QUARTERS[2 + a]))
+            )
+        grouped1 = grouped_w(1)
+        nc.scalar.copy(*by_fours(grouped1[:], 1))
 
-        h = {}
-        terms = {}
+        h = {0: sbuf("h0", [P, S], F32)}
 
-        def project(m, tile, banks):
-            h[m] = tile
-            low = bank(banks[0], [P, HALF], f"h_low{m}")
-            product(low[:], *w_mx[m], x_codes[:, HALVES[0]], x_plane[:, HALVES[0]])
-            nc.scalar.copy(out=tile[:, HALVES[0]], in_=low[:])
-            high = bank(banks[1], [P, HALF], f"h_high{m}")
-            product(high[:, 0:P], *w_mx[m], x_codes[:, HALF : EARLY.stop], x_plane[:, HALF : EARLY.stop])
-            product(high[:, P:HALF], *w_mx[m], x_codes[:, LATE], x_plane_late[:])
-            nc.scalar.copy(out=tile[:, HALVES[1]], in_=high[:])
+        def project(m, acc, a):
+            product(acc, *w_mx[m], x_codes[:, HALVES[a]], x_planes[a][:])
+
+        low = bank(0, [P, HALF], "h0_low")
+        project(0, low[:], 0)
+        nc.scalar.copy(out=h[0][:, HALVES[0]], in_=low[:])
+        for a in range(2):
+            part = bank((1, 6)[a], [P, P], f"h0_high{a}")
+            product(part[:], *w_mx[0], x_codes[:, QUARTERS[2 + a]], x_planes[1][:, BLOCKS[a]])
+            nc.scalar.copy(out=h[0][:, QUARTERS[2 + a]], in_=part[:])
+
+        h_ps = {}
+
+        def project_whole(m, number):
+            h_ps[m] = bank(number, [P, S], f"h{m}_ps")
+            for a in range(2):
+                project(m, h_ps[m][:, HALVES[a]], a)
+
+        def leave_bank(m, after=None):
+            h[m] = sbuf(f"h{m}", [P, S], F32, after)
+            nc.scalar.copy(out=h[m][:], in_=h_ps[m][:])
+
+        def fetch(m, d, part, cols=ALL):
+            nc.scalar.activation(out=part, in_=h[m][:].indirect(entries(pos_t[d], cols)), func=COPY)
 
         def gather_term(m, d, cols, part):
             nc.vector.tensor_tensor(
-                out=part, in0=h[m][:].indirect(entries(pos_t[d], cols)), in1=gate_t[:, d, cols], op=MULT
+                out=part, in0=h[m][:].indirect(entries(pos_t[d], cols)), in1=gates[d][:, cols], op=MULT
             )
 
-        def fetch(m, part):
-            nc.scalar.activation(out=part, in_=h[m][:].indirect(pos_t[D - 1][:]), func=COPY)
+        def weigh(m):
+            count = fetched[m].shape[1]
+            terms = sbuf(f"weighed{m}", [P, count, V], F32, "w_raw3" if m == 0 else None)
+            nc.vector.tensor_tensor(out=terms[:], in0=fetched[m][:], in1=gate_t[:, D - count :, :], op=MULT)
+            return terms
 
-        def add_turned(sums, part, start, stop):
-            nc.tensor.matmul(out=sums, lhsT=part, rhs=ident[:], is_transpose=True, start=start, stop=stop)
+        def add_turned(sums_out, part, start, stop):
+            nc.tensor.matmul(out=sums_out, lhsT=part, rhs=ident[:], is_transpose=True, start=start, stop=stop)
 
-        sums = [bank(2 + b, [P, 3, P], f"sums{b}") for b in range(2)]
+        early = [bank(2, [P, 2, P], "early0"), bank(3, [P, 3, P], "early1")]
+        last = [bank(7, [P, 2, P], "last0"), bank(6, [P, P], "last1")]
+        home = {
+            0: (early[0][:, 0, :], early[1][:, 0, :]),
+            1: (early[0][:, 1, :], early[1][:, 1, :]),
+            2: (last[0][:, 0, :], early[1][:, 2, :]),
+            3: (last[0][:, 1, :], last[1][:]),
+        }
 
-        def add_term(m, part, start=False, stop=False):
+        def add_term(m, part, start=(False, False), stop=(False, False)):
             for b in range(2):
-                add_turned(sums[b][:, m, :], part[:, BLOCKS[b]], start, stop)
+                add_turned(home[m][b], part[:, BLOCKS[b]], start[b], stop[b])
 
-        def fused(m, d, part=None, start=False):
-            if part is None:
-                part = sbuf(f"term{m}_{d}", [P, V], F32)[:]
-            gather_term(m, d, ALL, part)
-            terms[m, d] = part
-            add_term(m, part, start=start)
+        def fused(m, d, start=(False, False)):
+            part = sbuf(f"term{m}_{d}", [P, V], F32)
+            gather_term(m, d, ALL, part[:])
+            add_term(m, part[:], start=start)
+            return part
 
-        def weigh(name, fetched, count):
-            term = sbuf(name, [P, count, V], F32)
-            nc.vector.tensor_tensor(
-                out=term[:], in0=fetched, in1=gate_t[:, D - 1 : D, :].to_broadcast([P, count, V]), op=MULT
-            )
-            return term
+        def weighed(m, stop=(False, False)):
+            terms = weigh(m)
+            count = terms.shape[1]
+            for c in range(count):
+                add_term(m, terms[:, c, :], stop=stop if c == count - 1 else (False, False))
+            return terms
 
-        project(0, sbuf("h0", [P, S], F32), (0, 1))
-        w_mx[1] = quantise("w1", grouped1)
+        quantise_w(1, grouped1)
+        project_whole(1, 4)
         v_rows = sbuf("v_rows", [P, R], U8, "w_raw1")
         nc.vector.tensor_copy(out=v_rows[:], in_=v_table_rows[:].indirect(cand_t[:]))
-        project(1, sbuf("h1", [P, S], F32), (4, 5))
-
-        grouped2 = sbuf("w_grouped2", [P, P, PACK], BF16)
+        grouped2 = grouped_w(2, "w_grouped1")
         nc.gpsimd.tensor_scalar(
             out=grouped2[:], in0=w_raw[2][:].rearrange("p j c -> p c j"), scalar1=1.0, scalar2=0.0, op0=MULT, op1=ADD
         )
-        w_mx[2] = quantise("w2", grouped2, plane_at=PLANE2_AT)
-        first_terms = sbuf("first_terms", [P, 2, V], F32, "w_raw2")
-        fused(0, 0, first_terms[:, 0, :], start=True)
-        fused(1, 0, first_terms[:, 1, :])
-        fused(0, 1)
-        fetched0 = sbuf("fetched0", [P, 1, V], F32)
-        fetch(0, fetched0[:, 0, :])
-        add_term(0, weigh("term0_2", fetched0[:], 1)[:, 0, :])
-        grouped3 = cast_w(3)
-        project(2, placed("h2", [P, S], H2_AT), (0, 1))
-        w_mx[3] = quantise("w3", grouped3)
-        v_plane = sbuf("v_plane", [P, R], U8, "w2_codes")
+        quantise_w(2, grouped2, plane_at=PLANE2_AT)
+        project_whole(2, 5)
+        grouped3 = grouped_w(3)
+        nc.vector.tensor_copy(*by_fours(grouped3[:], 3))
+        fetched = {0: sbuf("fetched0", [P, 2, V], F32)}
+        fetch(0, 1, fetched[0][:, 0, :])
+        leave_bank(1)
+        fetch(0, 2, fetched[0][:, 1, :])
+        leave_bank(2)
+        t00 = fused(0, 0, start=(True, True))
+        quantise_w(3, grouped3, plane_at=PLANE3_AT)
+        project_whole(3, 0)
+        t10 = fused(1, 0)
+        fetched[1] = placed("fetched1", [P, 2, V], FETCHED1_AT)
+        fetch(1, 1, fetched[1][:, 0, :])
+        fetch(1, 2, fetched[1][:, 1, :])
+        leave_bank(3)
+        fetched[2] = placed("fetched2", [P, 1, V], FETCHED2_AT)
+        fetch(2, 2, fetched[2][:, 0, :])
+        fetched3 = [sbuf(f"fetched3_block{b}", [P, P], F32) for b in range(2)]
+        fetched21 = sbuf("fetched2_1_block1", [P, P], F32)
+        fetch(3, 2, fetched3[0][:], BLOCKS[0])
+        fetch(2, 1, fetched21[:], BLOCKS[1])
+        fetch(3, 2, fetched3[1][:], BLOCKS[1])
+        v_plane = sbuf("v_plane", [P, R], U8, "w_codes3")
         spread_scale_rows(nc, v_plane, v_rows[0:P:ROW_STEP, :])
-        fused(1, 1, placed("term1_1", [P, V], TERM11_AT)[:])
-        fetched12 = placed("fetched12", [P, V + P + V], FETCHED_AT)
-        fetch(1, fetched12[:, 0:V])
-        nc.scalar.activation(out=fetched12[:, V : V + P], in_=h[2][:].indirect(entries(pos_t[1], BLOCKS[1])), func=COPY)
-        fetch(2, fetched12[:, V + P :])
-        project(3, sbuf("h3", [P, S], F32), (1, 0))
-        fused(2, 0)
-        term21 = sbuf("term2_1_block0", [P, P], F32)
-        gather_term(2, 1, BLOCKS[0], term21[:])
-        add_turned(sums[0][:, 2, :], term21[:], False, False)
-        add_term(1, weigh("term1_2", fetched12[:, 0:V].rearrange("p (o t) -> p o t", o=1), 1)[:, 0, :])
-        terms12 = sbuf("terms2", [P, P + V], F32)
-        nc.vector.tensor_tensor(
-            out=terms12[:], in0=fetched12[:, V:], in1=gate_t[:].rearrange("p d t -> p (d t)")[:, V + P :], op=MULT
-        )
-        add_turned(sums[1][:, 2, :], terms12[:, 0:P], False, False)
-        add_term(2, terms12[:, P:], stop=True)
-        fetched3 = sbuf("fetched3", [P, 1, V], F32)
-        fetch(3, fetched3[:, 0, :])
+        w0 = weighed(0)
+        t20 = fused(2, 0, start=(True, False))
+        t21 = sbuf("term2_1_block0", [P, P], F32)
+        gather_term(2, 1, BLOCKS[0], t21[:])
+        add_turned(home[2][0], t21[:], False, False)
+        w1_ = weighed(1, stop=(True, False))
 
-        zt = [sbuf(f"zt{b}", [P, 2, P, 2], BF16) for b in range(2)]
+        zt = {0: sbuf("zt0", [P, 2, P, 2], BF16)}
 
         def round_z(b, first, sums_in):
             count = sums_in.shape[1] // PACK
@@ -251,22 +275,32 @@ def tile_picked_zcbow_sig_p_kernel(
                 in_=sums_in.rearrange("t (p u e) -> t u p e", u=2, e=2),
             )
 
-        for b in range(2):
-            round_z(b, 0, sums[b][:].rearrange("t m i -> t (m i)"))
 
-        last = [bank(6 + b, [P, P], f"last{b}") for b in range(2)]
-        first_parts = [placed("term3_0_block0", [P, P], TERM30_AT), sbuf("term3_1_block0", [P, P], F32)]
-        for d in range(2):
-            gather_term(3, d, BLOCKS[0], first_parts[d][:])
-            add_turned(last[0][:], first_parts[d][:], d == 0, False)
-        term3_2 = weigh("term3_2", fetched3[:], 1)
-        add_turned(last[0][:], term3_2[:, 0, BLOCKS[0]], False, True)
-        add_turned(last[1][:], term3_2[:, 0, BLOCKS[1]], True, False)
-        round_z(0, 3 * P // PACK, last[0][:])
-        second_parts = [placed("term3_0_block1", [P, P], TERM30_LATE_AT), placed("term3_1_block1", [P, P], TERM31_LATE_AT)]
-        for d in range(2):
-            gather_term(3, d, BLOCKS[1], second_parts[d][:])
-            add_turned(last[1][:], second_parts[d][:], False, d == 1)
+        def last_term(d, b, part, start=False, stop=False):
+            gather_term(3, d, BLOCKS[b], part[:])
+            add_turned(home[3][b], part[:], start, stop)
+
+        last_term(0, 0, sbuf("term3_0_block0", [P, P], F32))
+        last_term(1, 0, placed("term3_1_block0", [P, P], TERM31_AT))
+        w2 = weighed(2)
+        round_z(0, 0, early[0][:].rearrange("t m i -> t (m i)"))
+
+        def last_weighed(b):
+            part = sbuf(f"term3_2_block{b}", [P, P], F32)
+            nc.vector.tensor_tensor(out=part[:], in0=fetched3[b][:], in1=gates[D - 1][:, BLOCKS[b]], op=MULT)
+            add_turned(home[3][b], part[:], False, True)
+            return part
+
+        last_weighed(0)
+        round_z(0, 2 * P // PACK, last[0][:].rearrange("t m i -> t (m i)"))
+        last_term(0, 1, sbuf("term3_0_block1", [P, P], F32), start=True)
+        term21 = sbuf("term2_1_block1", [P, P], F32)
+        nc.vector.tensor_tensor(out=term21[:], in0=fetched21[:], in1=gates[1][:, BLOCKS[1]], op=MULT)
+        add_turned(home[2][1], term21[:], False, True)
+        zt[1] = sbuf("zt1", [P, 2, P, 2], BF16, "term3_2_block0")
+        round_z(1, 0, early[1][:].rearrange("t m i -> t (m i)"))
+        last_term(1, 1, sbuf("term3_1_block1", [P, P], F32))
+        tl = last_weighed(1)
         round_z(1, 3 * P // PACK, last[1][:])
 
         def turn_z(b, number, pieces):
@@ -283,6 +317,12 @@ def tile_picked_zcbow_sig_p_kernel(
         window_halves = (slice(0, P // 2), slice(P // 2, P))
         z_grouped = [turn_z(0, 0, [slice(0, P)]), turn_z(1, 1, window_halves)]
 
+        def quantise_z(b, pieces):
+            codes, plane = sbuf(f"z_codes{b}", [P, P], U32), sbuf(f"z_plane{b}", [P, P], U8)
+            for part in pieces:
+                quantise(codes[:, part], plane[:, part], z_grouped[b][:, part, :])
+            return codes[:], plane[:]
+
         def score(z_mx, cols, number, result):
             y_ps = bank(number, [P, cols.stop - cols.start], f"y_ps{number}")
             product(y_ps[:], *z_mx, v_codes[:, cols], v_plane[:, cols])
@@ -293,14 +333,14 @@ def tile_picked_zcbow_sig_p_kernel(
 
         v_codes = placed("v_codes", [P, R], V_CODES_AT, U32)
         nc.vector.tensor_copy(out=v_codes[:], in_=v_table[:].indirect(cand_t[:]))
-        z0 = quantise("z0", z_grouped[0])
-        result0 = sbuf("result0", [P, R], F32, "zt1")
+        z0 = quantise_z(0, [slice(0, P)])
+        result0 = sbuf("result0", [P, R], F32, "term3_2_block0")
         score(z0, slice(0, P), 4, result0)
         score(z0, slice(P, HALF), 5, result0)
         store(0, HALVES[0], result0)
         score(z0, HALVES[1], 6, result0)
         store(0, HALVES[1], result0)
-        z1 = quantise("z1", z_grouped[1], window_halves)
+        z1 = quantise_z(1, window_halves)
         result1 = sbuf("result1", [P, R], F32)
         for a, cols in enumerate(HALVES):
             score(z1, slice(cols.start, cols.start + P), (2, 7)[a], result1)

@@ -35,7 +35,7 @@ PLANE2_AT = 2 * KIB
 FETCHED1_AT = PLANE2_AT - 2 * KIB + EDGE
 PLANE3_AT = 4 * KIB
 FETCHED2_AT = PLANE3_AT - KIB + EDGE
-TERM31_AT = 8 * KIB
+TERM31_AT = 12 * KIB
 V_CODES_AT = TERM31_AT - 2 * KIB + EDGE
 
 
@@ -250,13 +250,9 @@ def tile_picked_zcbow_sig_p_kernel(
         fetch(1, 1, fetched[1][:, 0, :])
         fetch(1, 2, fetched[1][:, 1, :])
         leave_bank(3)
-        fetched[2] = placed("fetched2", [P, 1, V], FETCHED2_AT)
-        fetch(2, 2, fetched[2][:, 0, :])
-        fetched3 = [sbuf(f"fetched3_block{b}", [P, P], F32) for b in range(2)]
-        fetched21 = sbuf("fetched2_1_block1", [P, P], F32)
-        fetch(3, 2, fetched3[0][:], BLOCKS[0])
-        fetch(2, 1, fetched21[:], BLOCKS[1])
-        fetch(3, 2, fetched3[1][:], BLOCKS[1])
+        late0 = placed("late0", [P, 2, P], FETCHED2_AT)
+        for m in (2, 3):
+            fetch(m, 2, late0[:, m - 2, :], BLOCKS[0])
         v_plane = sbuf("v_plane", [P, R], U8, "w_codes3")
         spread_scale_rows(nc, v_plane, v_rows[0:P:ROW_STEP, :])
         w0 = weighed(0)
@@ -265,6 +261,10 @@ def tile_picked_zcbow_sig_p_kernel(
         gather_term(2, 1, BLOCKS[0], t21[:])
         add_turned(home[2][0], t21[:], False, False)
         w1_ = weighed(1, stop=(True, False))
+        late1 = sbuf("late1", [P, 2, 2, P], F32, "w_raw3")
+        for m in (2, 3):
+            for d in (1, 2):
+                fetch(m, d, late1[:, m - 2, d - 1, :], BLOCKS[1])
 
         zt = {0: sbuf("zt0", [P, 2, P, 2], BF16)}
 
@@ -282,25 +282,26 @@ def tile_picked_zcbow_sig_p_kernel(
 
         last_term(0, 0, sbuf("term3_0_block0", [P, P], F32))
         last_term(1, 0, placed("term3_1_block0", [P, P], TERM31_AT))
-        w2 = weighed(2)
         round_z(0, 0, early[0][:].rearrange("t m i -> t (m i)"))
 
-        def last_weighed(b):
-            part = sbuf(f"term3_2_block{b}", [P, P], F32)
-            nc.vector.tensor_tensor(out=part[:], in0=fetched3[b][:], in1=gates[D - 1][:, BLOCKS[b]], op=MULT)
-            add_turned(home[3][b], part[:], False, True)
-            return part
+        def weigh_late(name, fetched_part, weights):
+            terms = sbuf(name, list(fetched_part.shape), F32)
+            nc.vector.tensor_tensor(out=terms[:], in0=fetched_part, in1=weights, op=MULT)
+            return terms
 
-        last_weighed(0)
+        terms0 = weigh_late("late_terms0", late0[:], gate_t[:, 2:, BLOCKS[0]].to_broadcast([P, 2, P]))
+        for m in (2, 3):
+            add_turned(home[m][0], terms0[:, m - 2, :], False, m == 3)
         round_z(0, 2 * P // PACK, last[0][:].rearrange("t m i -> t (m i)"))
         last_term(0, 1, sbuf("term3_0_block1", [P, P], F32), start=True)
-        term21 = sbuf("term2_1_block1", [P, P], F32)
-        nc.vector.tensor_tensor(out=term21[:], in0=fetched21[:], in1=gates[1][:, BLOCKS[1]], op=MULT)
-        add_turned(home[2][1], term21[:], False, True)
-        zt[1] = sbuf("zt1", [P, 2, P, 2], BF16, "term3_2_block0")
+        terms2 = weigh_late("late_terms2", late1[:, 0], gate_t[:, 1:, BLOCKS[1]])
+        for c in range(2):
+            add_turned(home[2][1], terms2[:, c, :], False, c == 1)
+        zt[1] = sbuf("zt1", [P, 2, P, 2], BF16)
         round_z(1, 0, early[1][:].rearrange("t m i -> t (m i)"))
-        last_term(1, 1, sbuf("term3_1_block1", [P, P], F32))
-        tl = last_weighed(1)
+        for d in (1, 2):
+            tl = weigh_late(f"late_term3_{d}", late1[:, 1, d - 1, :], gates[d][:, BLOCKS[1]])
+            add_turned(home[3][1], tl[:], False, d == 2)
         round_z(1, 3 * P // PACK, last[1][:])
 
         def turn_z(b, number, pieces):
@@ -334,7 +335,7 @@ def tile_picked_zcbow_sig_p_kernel(
         v_codes = placed("v_codes", [P, R], V_CODES_AT, U32)
         nc.vector.tensor_copy(out=v_codes[:], in_=v_table[:].indirect(cand_t[:]))
         z0 = quantise_z(0, [slice(0, P)])
-        result0 = sbuf("result0", [P, R], F32, "term3_2_block0")
+        result0 = sbuf("result0", [P, R], F32, "zt1")
         score(z0, slice(0, P), 4, result0)
         score(z0, slice(P, HALF), 5, result0)
         store(0, HALVES[0], result0)

@@ -108,13 +108,13 @@ def tile_picked_zcbow_sig_p_kernel(
         def load_w(m):
             nc.sync.dma_start(out=w_raw[m][:], in_=w_rows[:, :, m * P : (m + 1) * P])
 
-        nc.sync.dma_start(out=x_table[:].bitcast(I32), in_=as_words(x_words))
         nc.sync.dma_start(out=offs_t[:], in_=offs)
+        nc.sync.dma_start(out=x_table[:].bitcast(I32), in_=as_words(x_words))
         spread_scale_rows(nc, x_table_plane, x_scales[0])
         load_w(0)
         load_w(1)
-        nc.sync.dma_start(out=pos_t[1][:], in_=pos2)
         load_w(2)
+        nc.sync.dma_start(out=pos_t[1][:], in_=pos2)
         nc.sync.dma_start(out=cand_t[:], in_=cand)
         nc.sync.dma_start(out=pos_t[2][:], in_=pos3)
         nc.sync.dma_start(out=gate_t[:], in_=gate.rearrange("d p t -> p d t"))
@@ -227,14 +227,14 @@ def tile_picked_zcbow_sig_p_kernel(
 
         quantise_w(1, grouped1)
         project_whole(1, 4)
-        v_rows = sbuf("v_rows", [P, R], U8, "w_raw1")
-        nc.vector.tensor_copy(out=v_rows[:], in_=v_table_rows[:].indirect(cand_t[:]))
-        grouped2 = grouped_w(2, "w_grouped1")
+        grouped2 = grouped_w(2)
         nc.gpsimd.tensor_scalar(
             out=grouped2[:], in0=w_raw[2][:].rearrange("p j c -> p c j"), scalar1=1.0, scalar2=0.0, op0=MULT, op1=ADD
         )
         quantise_w(2, grouped2, plane_at=PLANE2_AT)
         project_whole(2, 5)
+        v_rows = sbuf("v_rows", [P, R], U8, "w_raw1")
+        nc.vector.tensor_copy(out=v_rows[:], in_=v_table_rows[:].indirect(cand_t[:]))
         grouped3 = grouped_w(3)
         nc.vector.tensor_copy(*by_fours(grouped3[:], 3))
         fetched = {0: sbuf("fetched0", [P, 2, V], F32)}

@@ -117,9 +117,9 @@ def tile_picked_zcbow_sig_p_kernel(
         nc.sync.dma_start(out=pos_t[1][:], in_=pos2)
         nc.sync.dma_start(out=cand_t[:], in_=cand)
         nc.sync.dma_start(out=pos_t[2][:], in_=pos3)
-        nc.sync.dma_start(out=gate_t[:], in_=gate.rearrange("d p t -> p d t"))
         load_w(3)
         nc.sync.dma_start(out=pos_t[0][:], in_=pos1)
+        nc.sync.dma_start(out=gate_t[:], in_=gate.rearrange("d p t -> p d t"))
         nc.sync.dma_start(out=v_table[:].bitcast(I32), in_=as_words(v_words))
 
         nc.scalar.activation(out=warm[:, 1:2], in_=warm[:, 0:1], func=SIGMOID)

@@ -108,8 +108,8 @@ def tile_picked_zcbow_sig_p_kernel(
         def load_w(m):
             nc.sync.dma_start(out=w_raw[m][:], in_=w_rows[:, :, m * P : (m + 1) * P])
 
-        nc.sync.dma_start(out=offs_t[:], in_=offs)
         nc.sync.dma_start(out=x_table[:].bitcast(I32), in_=as_words(x_words))
+        nc.sync.dma_start(out=offs_t[:], in_=offs)
         spread_scale_rows(nc, x_table_plane, x_scales[0])
         load_w(0)
         load_w(1)

from contextlib import ExitStack

import concourse.mybir as mybir
from concourse.masks import make_identity

K, T, S, D, V, H, G, R = 512, 1024, 512, 3, 256, 512, 2048, 512
FLOPS = 2 * K * H * S + 2 * H * V * R

F32 = mybir.dt.float32
BF16 = mybir.dt.bfloat16
I32 = mybir.dt.int32
U32 = mybir.dt.uint32
U16 = mybir.dt.uint16
U8 = mybir.dt.uint8
FP8X4 = mybir.dt.float8_e4m3fn_x4
MULT = mybir.AluOpType.mult
ADD = mybir.AluOpType.add
SIGMOID = mybir.ActivationFunctionType.Sigmoid
COPY = mybir.ActivationFunctionType.Copy

P = 128
PACK = 4
QUADRANT = 32
SCALE_ROWS = 16
ROW_STEP = P // SCALE_ROWS
LIST_ROWS = 16
HALF = 256
HALVES = (slice(0, HALF), slice(HALF, 2 * HALF))
BLOCKS = (slice(0, P), slice(P, V))
ALL = slice(0, V)
QUARTERS = tuple(slice(a * P, (a + 1) * P) for a in range(4))
KIB = 1024
EDGE = 64
PLANE2_AT = 2 * KIB
FETCHED1_AT = PLANE2_AT - 2 * KIB + EDGE
PLANE3_AT = 4 * KIB
FETCHED2_AT = PLANE3_AT - KIB + EDGE
TERM31_AT = 12 * KIB
V_CODES_AT = TERM31_AT - 2 * KIB + EDGE


def as_words(words):
    return words[0].rearrange("p n t -> p (n t)").bitcast(I32)


def spread_scale_rows(nc, plane, rows):
    for r in range(PACK):
        nc.sync.dma_start(out=plane[r:P:QUADRANT, :].bitcast(I32), in_=rows[r:SCALE_ROWS:PACK, :].bitcast(I32))


def entries(offsets, cols):
    return offsets[:, cols.start // LIST_ROWS : cols.stop // LIST_ROWS]


def tile_picked_zcbow_sig_p_kernel(
    tc, x_words, x_scales, w1, gate, v_words, v_scales, offs, pos1, pos2, pos3, cand, out
):
    nc = tc.nc
    with ExitStack() as ctx:
        keep = ctx.enter_context(tc.tile_pool(name="keep", bufs=1))
        shared = ctx.enter_context(tc.tile_pool(name="shared", bufs=1))
        psum = ctx.enter_context(tc.psum_pool(name="psum", bufs=1))

        def sbuf(name, shape, dtype, after=None):
            return keep.tile(shape, dtype, name=name, tag=after or name, align_bytes=64)

        def placed(name, shape, offset, dtype=F32):
            return shared.tile(shape, dtype, name=name, offset=offset, align_bytes=64)

        def bank(number, shape, name):
            return psum.tile(shape, F32, name=name, tag=f"bank{number}")

        def product(acc, codes, plane, moving, moving_plane):
            nc.tensor.matmul_mx(
                out=acc,
                lhsT=codes.bitcast(FP8X4),
                lhsT_scale=plane,
                rhs=moving.bitcast(FP8X4),
                rhs_scale=moving_plane,
                start=True,
                stop=True,
            )

        def quantise(codes, plane, grouped):
            nc.vector.quantize_mx(out=codes.bitcast(FP8X4), scales=plane, in_=grouped.rearrange("p c j -> p (c j)"))

        offs_t = sbuf("offs_t", [P, S // LIST_ROWS], U16)
        cand_t = sbuf("cand_t", [P, R // LIST_ROWS], U16)
        pos_t = [sbuf(f"pos_t{d}", [P, V // LIST_ROWS], U16) for d in range(D)]
        x_table = sbuf("x_table", [P, T], U32)
        x_table_plane = sbuf("x_table_plane", [P, T], U8)
        v_table = sbuf("v_table", [P, G], U32)
        v_table_rows = sbuf("v_table_rows", [P, G], U8)
        gate_t = sbuf("gate_t", [P, D, V], F32)
        gates = [gate_t[:, d, :] for d in range(D)]
        w_raw = [sbuf(f"w_raw{m}", [P, PACK, P], F32) for m in range(PACK)]
        ident = sbuf("ident", [P, P], F32)
        warm = sbuf("warm", [P, 8], F32)

        nc.gpsimd.memset(x_table_plane[:].bitcast(I32), 0)
        nc.gpsimd.memset(warm[:], 0.0)
        nc.gpsimd.memset(v_table_rows[:].bitcast(I32), 0)
        nc.gpsimd.dma_start(out=v_table_rows[0:P:ROW_STEP, :].bitcast(I32), in_=v_scales[0].bitcast(I32))
        make_identity(nc, ident[:])

        w_rows = w1.rearrange("(p j) c -> p j c", j=PACK)

        def load_w(m):
            nc.sync.dma_start(out=w_raw[m][:], in_=w_rows[:, :, m * P : (m + 1) * P])

        nc.sync.dma_start(out=x_table[:].bitcast(I32), in_=as_words(x_words))
        nc.sync.dma_start(out=offs_t[:], in_=offs)
        spread_scale_rows(nc, x_table_plane, x_scales[0])
        load_w(0)
        load_w(1)
        load_w(2)
        nc.sync.dma_start(out=pos_t[1][:], in_=pos2)
        nc.sync.dma_start(out=cand_t[:], in_=cand)
        nc.sync.dma_start(out=pos_t[2][:], in_=pos3)
        load_w(3)
        nc.sync.dma_start(out=pos_t[0][:], in_=pos1)
        nc.sync.dma_start(out=gate_t[:], in_=gate.rearrange("d p t -> p d t"))
        nc.sync.dma_start(out=v_table[:].bitcast(I32), in_=as_words(v_words))

        nc.scalar.activation(out=warm[:, 1:2], in_=warm[:, 0:1], func=SIGMOID)

        def by_fours(grouped, m):
            return (
                grouped.rearrange("p (c i) j -> p c j i", i=PACK),
                w_raw[m][:].rearrange("p j (c i) -> p c j i", i=PACK),
            )

        w_mx = {}

        def grouped_w(m, after=None):
            return sbuf(f"w_grouped{m}", [P, P, PACK], BF16, after)

        def quantise_w(m, grouped, plane_at=None, after=None):
            codes = sbuf(f"w_codes{m}", [P, P], U32, after)
            if plane_at is None:
                plane = sbuf(f"w_plane{m}", [P, P], U8)
            else:
                plane = placed(f"w_plane{m}", [P, P], plane_at, U8)
            quantise(codes[:], plane[:], grouped[:])
            w_mx[m] = (codes[:], plane[:])

        x_codes = sbuf("x_codes", [P, S], U32)
        nc.vector.tensor_copy(out=x_codes[:], in_=x_table[:].indirect(offs_t[:]))
        x_planes = [sbuf("x_plane0", [P, HALF], U8), sbuf("x_plane1", [P, HALF], U8, "w_raw0")]
        nc.vector.tensor_copy(out=x_planes[0][:], in_=x_table_plane[:].indirect(entries(offs_t, HALVES[0])))
        grouped0 = grouped_w(0)
        nc.scalar.copy(*by_fours(grouped0[:], 0))
        quantise_w(0, grouped0)
        for a in range(2):
            nc.vector.tensor_copy(
                out=x_planes[1][:, BLOCKS[a]], in_=x_table_plane[:].indirect(entries(offs_t, QUARTERS[2 + a]))
            )
        grouped1 = grouped_w(1)
        nc.scalar.copy(*by_fours(grouped1[:], 1))

        h = {0: sbuf("h0", [P, S], F32)}

        def project(m, acc, a):
            product(acc, *w_mx[m], x_codes[:, HALVES[a]], x_planes[a][:])

        low = bank(0, [P, HALF], "h0_low")
        project(0, low[:], 0)
        nc.scalar.copy(out=h[0][:, HALVES[0]], in_=low[:])
        for a in range(2):
            part = bank((1, 6)[a], [P, P], f"h0_high{a}")
            product(part[:], *w_mx[0], x_codes[:, QUARTERS[2 + a]], x_planes[1][:, BLOCKS[a]])
            nc.scalar.copy(out=h[0][:, QUARTERS[2 + a]], in_=part[:])

        h_ps = {}

        def project_whole(m, number):
            h_ps[m] = bank(number, [P, S], f"h{m}_ps")
            for a in range(2):
                project(m, h_ps[m][:, HALVES[a]], a)

        def leave_bank(m, after=None):
            h[m] = sbuf(f"h{m}", [P, S], F32, after)
            nc.scalar.copy(out=h[m][:], in_=h_ps[m][:])

        def fetch(m, d, part, cols=ALL):
            nc.scalar.activation(out=part, in_=h[m][:].indirect(entries(pos_t[d], cols)), func=COPY)

        def gather_term(m, d, cols, part):
            nc.vector.tensor_tensor(
                out=part, in0=h[m][:].indirect(entries(pos_t[d], cols)), in1=gates[d][:, cols], op=MULT
            )

        def weigh(m):
            count = fetched[m].shape[1]
            terms = sbuf(f"weighed{m}", [P, count, V], F32, "w_raw3" if m == 0 else None)
            nc.vector.tensor_tensor(out=terms[:], in0=fetched[m][:], in1=gate_t[:, D - count :, :], op=MULT)
            return terms

        def add_turned(sums_out, part, start, stop):
            nc.tensor.matmul(out=sums_out, lhsT=part, rhs=ident[:], is_transpose=True, start=start, stop=stop)

        early = [bank(2, [P, 2, P], "early0"), bank(3, [P, 3, P], "early1")]
        last = [bank(7, [P, 2, P], "last0"), bank(6, [P, P], "last1")]
        home = {
            0: (early[0][:, 0, :], early[1][:, 0, :]),
            1: (early[0][:, 1, :], early[1][:, 1, :]),
            2: (last[0][:, 0, :], early[1][:, 2, :]),
            3: (last[0][:, 1, :], last[1][:]),
        }

        def add_term(m, part, start=(False, False), stop=(False, False)):
            for b in range(2):
                add_turned(home[m][b], part[:, BLOCKS[b]], start[b], stop[b])

        def fused(m, d, start=(False, False)):
            part = sbuf(f"term{m}_{d}", [P, V], F32)
            gather_term(m, d, ALL, part[:])
            add_term(m, part[:], start=start)
            return part

        def weighed(m, stop=(False, False)):
            terms = weigh(m)
            count = terms.shape[1]
            for c in range(count):
                add_term(m, terms[:, c, :], stop=stop if c == count - 1 else (False, False))
            return terms

        quantise_w(1, grouped1)
        project_whole(1, 4)
        grouped2 = grouped_w(2)
        nc.gpsimd.tensor_scalar(
            out=grouped2[:], in0=w_raw[2][:].rearrange("p j c -> p c j"), scalar1=1.0, scalar2=0.0, op0=MULT, op1=ADD
        )
        quantise_w(2, grouped2, plane_at=PLANE2_AT)
        project_whole(2, 5)
        v_rows = sbuf("v_rows", [P, R], U8, "w_raw1")
        nc.vector.tensor_copy(out=v_rows[:], in_=v_table_rows[:].indirect(cand_t[:]))
        grouped3 = grouped_w(3)
        nc.vector.tensor_copy(*by_fours(grouped3[:], 3))
        fetched = {0: sbuf("fetched0", [P, 2, V], F32)}
        fetch(0, 1, fetched[0][:, 0, :])
        leave_bank(1)
        fetch(0, 2, fetched[0][:, 1, :])
        leave_bank(2)
        t00 = fused(0, 0, start=(True, True))
        quantise_w(3, grouped3, plane_at=PLANE3_AT)
        project_whole(3, 0)
        t10 = fused(1, 0)
        fetched[1] = placed("fetched1", [P, 2, V], FETCHED1_AT)
        fetch(1, 1, fetched[1][:, 0, :])
        fetch(1, 2, fetched[1][:, 1, :])
        leave_bank(3)
        late0 = placed("late0", [P, 2, P], FETCHED2_AT)
        for m in (2, 3):
            fetch(m, 2, late0[:, m - 2, :], BLOCKS[0])
        v_plane = sbuf("v_plane", [P, R], U8, "w_codes3")
        spread_scale_rows(nc, v_plane, v_rows[0:P:ROW_STEP, :])
        w0 = weighed(0)
        t20 = fused(2, 0, start=(True, False))
        t21 = sbuf("term2_1_block0", [P, P], F32)
        gather_term(2, 1, BLOCKS[0], t21[:])
        add_turned(home[2][0], t21[:], False, False)
        w1_ = weighed(1, stop=(True, False))
        late1 = sbuf("late1", [P, 2, 2, P], F32, "w_raw3")
        for m in (2, 3):
            for d in (1, 2):
                fetch(m, d, late1[:, m - 2, d - 1, :], BLOCKS[1])

        zt = {0: sbuf("zt0", [P, 2, P, 2], BF16)}

        def round_z(b, first, sums_in):
            count = sums_in.shape[1] // PACK
            nc.scalar.copy(
                out=zt[b][:, :, first : first + count, :],
                in_=sums_in.rearrange("t (p u e) -> t u p e", u=2, e=2),
            )


        def last_term(d, b, part, start=False, stop=False):
            gather_term(3, d, BLOCKS[b], part[:])
            add_turned(home[3][b], part[:], start, stop)

        last_term(0, 0, sbuf("term3_0_block0", [P, P], F32))
        last_term(1, 0, placed("term3_1_block0", [P, P], TERM31_AT))
        round_z(0, 0, early[0][:].rearrange("t m i -> t (m i)"))

        def weigh_late(name, fetched_part, weights):
            terms = sbuf(name, list(fetched_part.shape), F32)
            nc.vector.tensor_tensor(out=terms[:], in0=fetched_part, in1=weights, op=MULT)
            return terms

        terms0 = weigh_late("late_terms0", late0[:], gate_t[:, 2:, BLOCKS[0]].to_broadcast([P, 2, P]))
        for m in (2, 3):
            add_turned(home[m][0], terms0[:, m - 2, :], False, m == 3)
        round_z(0, 2 * P // PACK, last[0][:].rearrange("t m i -> t (m i)"))
        last_term(0, 1, sbuf("term3_0_block1", [P, P], F32), start=True)
        terms2 = weigh_late("late_terms2", late1[:, 0], gate_t[:, 1:, BLOCKS[1]])
        for c in range(2):
            add_turned(home[2][1], terms2[:, c, :], False, c == 1)
        zt[1] = sbuf("zt1", [P, 2, P, 2], BF16)
        round_z(1, 0, early[1][:].rearrange("t m i -> t (m i)"))
        for d in (1, 2):
            tl = weigh_late(f"late_term3_{d}", late1[:, 1, d - 1, :], gates[d][:, BLOCKS[1]])
            add_turned(home[3][1], tl[:], False, d == 2)
        round_z(1, 3 * P // PACK, last[1][:])

        def turn_z(b, number, pieces):
            pairs = zt[b][:].rearrange("t u p e -> t (u p e)").bitcast(F32)
            z_ps = bank(number, [P, 2, P], f"z_ps{b}")
            for u in range(2):
                nc.tensor.transpose(z_ps[:, u, :], pairs[:, u * P : (u + 1) * P], ident[:])
            grouped = sbuf(f"z_grouped{b}", [P, P, PACK], BF16)
            grouped_pairs = grouped[:].rearrange("p t j -> p (t j)").bitcast(F32).rearrange("p (t u) -> p t u", u=2)
            for part in pieces:
                nc.scalar.copy(out=grouped_pairs[:, part], in_=z_ps[:].rearrange("p u t -> p t u")[:, part])
            return grouped

        window_halves = (slice(0, P // 2), slice(P // 2, P))
        z_grouped = [turn_z(0, 0, [slice(0, P)]), turn_z(1, 1, window_halves)]

        def quantise_z(b, pieces):
            codes, plane = sbuf(f"z_codes{b}", [P, P], U32), sbuf(f"z_plane{b}", [P, P], U8)
            for part in pieces:
                quantise(codes[:, part], plane[:, part], z_grouped[b][:, part, :])
            return codes[:], plane[:]

        def score(z_mx, cols, number, result):
            y_ps = bank(number, [P, cols.stop - cols.start], f"y_ps{number}")
            product(y_ps[:], *z_mx, v_codes[:, cols], v_plane[:, cols])
            nc.scalar.activation(out=result[:, cols], in_=y_ps[:], func=SIGMOID)

        def store(b, cols, result):
            nc.sync.dma_start(out=out[b * P : (b + 1) * P, cols], in_=result[:, cols])

        v_codes = placed("v_codes", [P, R], V_CODES_AT, U32)
        nc.vector.tensor_copy(out=v_codes[:], in_=v_table[:].indirect(cand_t[:]))
        z0 = quantise_z(0, [slice(0, P)])
        result0 = sbuf("result0", [P, R], F32, "zt1")
        score(z0, slice(0, P), 4, result0)
        score(z0, slice(P, HALF), 5, result0)
        store(0, HALVES[0], result0)
        score(z0, HALVES[1], 6, result0)
        store(0, HALVES[1], result0)
        z1 = quantise_z(1, window_halves)
        result1 = sbuf("result1", [P, R], F32)
        for a, cols in enumerate(HALVES):
            score(z1, slice(cols.start, cols.start + P), (2, 7)[a], result1)
            score(z1, slice(cols.start + P, cols.stop), (3, 0)[a], result1)
            store(1, cols, result1)
